import numpy as np, ml_dtypes
CORES = [2,6,10,14,18,22,26,30]
N = 8
BF = ml_dtypes.bfloat16
def gentries(a):
    return np.ascontiguousarray(a.reshape(8, 16, -1).transpose(0, 2, 1)).reshape(8, -1)
def gtable(e):
    e = np.asarray(e); return np.ascontiguousarray(e.reshape(8, -1, 16).transpose(0, 2, 1)).reshape(128, -1).astype(np.int32)
V, D, T, RO, NEED = 1344, 3, 32, 2, 8
E = D * V
def graph(rng, sizes, kinds, stray):
    c = rng.choice(np.array(sizes), V); z = np.add.accumulate(c); i = np.arange(V)
    b = np.searchsorted(z, i, side="right"); a = (z - c)[b]; n = np.minimum(z[b], V) - a
    kind = rng.choice(np.array(kinds), V)[b]; back = a + np.where(kind == 2, rng.integers(0, n), 0)
    t = np.where(kind == 0, a + rng.integers(0, n, (D, V)), np.where(i + 1 < a + n, i + 1, back))
    t = np.where(rng.random((D, V)) < stray, rng.integers(0, V, (D, V)), t)
    line = rng.permutation(V); h = np.empty((D, V), np.int64); h[:, line] = line[t]
    q = np.empty((3, V), np.int64); q[:, line] = np.stack([b, i - a, n])
    return h, q
def spins(rng, lean):
    return np.minimum(np.maximum(rng.integers(-7, 8, (16, E)) + np.tile(lean, D), -7), 7)
def sevens(rng, *shape):
    return np.where(rng.random(shape) < 0.125, 6, 7)
def layers(rng, sizes, kinds, strays, step):
    x = np.empty((N, 8, 16, E), np.int64); h = np.empty((N, 8, D, V), np.int64)
    for r in range(N):
        for g in range(8):
            h[r, g], q = graph(rng, sizes, kinds, rng.choice(np.array(strays)))
            x[r, g] = spins(rng, rng.integers(-step, step + 1, V)[q[0]])
    return x, np.argsort(rng.random((N, 8, E)), axis=-1), h
def pack(x, o, h):
    s = np.empty((N, 8, 16, E), np.int64); np.put_along_axis(s, np.ascontiguousarray(np.broadcast_to(o[:, :, None, :], s.shape)), x, 3)
    e = np.empty((N, 8, E), np.int64); np.put_along_axis(e, o, h.reshape(N, 8, E), 2)
    return {"sp": s.reshape(N, 128, E).astype(np.float32).astype(BF), "lv": np.stack([gtable(a) for a in o]), "hd": e.astype(np.int32)}
SIZES = (1, 2, 3, 5, 8, 13, 21, 34, T, T + 9)
def setup_inputs(rng):
    return pack(*layers(rng, SIZES, (0, 0, 0, 1, 1, 2), (0.0, 0.01, 0.04), 2))
def setup_inputs_length(rng):
    x, o, h = layers(rng, (1, T // 2, T - 1, T, T, T + 1, T + 1, 2 * T, 3 * T), (1, 1, 2), (0.0,), 3)
    for r in (0, N - 1):
        for g, c in enumerate((T, T + 1, T - 1, 2 * T, T // 2 + 1, 2, 256 + T // 2)):
            h[r, g], q = graph(rng, (c,), (1,), 0.0); x[r, g] = spins(rng, np.full(V, 3))
        line = np.concatenate([np.zeros(1, np.int64), 1 + rng.permutation(V - 1)]); to = np.empty(V, np.int64)
        to[line[1:]] = line[:-1]; to[0] = line[rng.integers(0, T // 2)]
        h[r, 7] = to; x[r, 7] = rng.integers(1, 8, (16, E))
    return pack(x, o, h)
def setup_inputs_verdict(rng):
    x, o, h = layers(rng, (1,), (1,), (0.0,), 0)
    for r in range(N):
        for g in range(8):
            h[r, g], q = graph(rng, (1, 2, 3, 4, 5, 8, 16), (1,), 0.0); b, j, n = q
            amp = rng.integers(-6, 7, (16, V))[:, b]; y = np.where(j % 2 == 1, -amp, amp)
            y = np.where((n % 2 == 1) & (j == n - 1), 0, y)
            won = np.argsort(rng.random((16, V)), axis=0) < rng.choice(np.array([NEED - 1, NEED, NEED, 0, 16]), V)
            want = np.where(won, 1, -rng.integers(0, 2, (16, V)))[:, b]
            x[r, g] = np.tile(y + np.where(j == 0, want, 0), (1, D))
    return pack(x, o, h)
def setup_inputs_ties(rng):
    x, o, h = layers(rng, (1, 2, 3, 5, 8), (0, 0, 1), (0.0, 0.01), 0)
    x[:, :2] = rng.choice(np.array([-7, -1, 0, 1, 2]), (N, 2, 1, E)); x[:, 2:4] = rng.integers(-1, 2, (N, 2, 16, E))
    x[:, 4:] = rng.integers(5, 8, (N, 4, 16, E)); near = np.array([7] * 6 + [5] * 7 + [6] * 3)
    for g in range(4, 8):
        y = x[:, g]; v = rng.permutation(V)[:V // 16]
        y[:, :, v] = 6; y[:, :, V + v] = rng.permutation(near)[:, None]
        for k in range(2, D): y[:, :, k * V + v] = 5
    x[:, 5::2] = -x[:, 5::2]
    return pack(x, o, h)
def setup_inputs_alike(rng):
    x, o, h = layers(rng, SIZES, (0, 1, 2), (0.0, 0.02), 2); i = np.arange(V)
    h[:, 0] = i; h[:, 1] = i ^ 1; h[:, 2] = 0; h[:, 3] = V - 1; h[:, 4] = np.roll(i, -1); h[:, 5] = rng.choice(np.array([0, V - 1]), (N, D, V))
    o[:, 6] = np.arange(E); o[:, 7] = np.arange(E)[::-1]
    r = int(rng.integers(0, N)); h[r] = i
    x[r] = sevens(rng, 8, 16, E); x[(r + 1) % N] = -sevens(rng, 8, 16, E); x[(r - 1) % N, :2] = sevens(rng, 2, 16, E)
    return pack(x, o, h)
def setup_inputs_spread(rng):
    x, o, h = layers(rng, (1, 2, 3, 4, 6, 9, 30), (0, 0, 1, 2), (0.0, 0.02), 0)
    size = rng.choice(np.array([0, 1, 1, 3, 7, 7]), (N, 8, 1, E)); sign = rng.choice(np.array([-1, 0, 1]), (N, 8, 1, E))
    v = np.rint((2 * rng.random((N, 8, 16, E)) - 1) * size).astype(np.int64)
    return pack(np.where(sign == 0, v, sign * np.abs(v)), o, h)
def check_inputs(d):
    bad = []; s = np.asarray(d["sp"]).astype(np.float32)
    if not (np.all(np.abs(s) <= 7) and np.all(s == np.rint(s))): bad.append("whole numbers of sp")
    if any(np.any(np.sort(gentries(a), axis=1) != np.arange(E)) for a in d["lv"]): bad.append("each edge once in lv")
    if np.min(d["hd"]) < 0 or np.max(d["hd"]) > V - 1: bad.append("range of hd")
    return bad
def reference(sp, lv, hd):
    s = sp.astype(np.float32).astype(np.int64).reshape(N, 8, 16, E); h = hd.astype(np.int64)
    o = np.stack([gentries(a) for a in lv]).astype(np.int64); me = np.arange(V); w = np.zeros((N, 8, 16, V), np.int64)
    for rnd in range(RO):
        so = np.take_along_axis(s, o[:, :, None, :], 3)
        a = np.add.reduce(so * np.roll(so, -1, axis=0), axis=2).reshape(N, 8, D, V)
        slot = np.argmax(a, axis=2) * V + me
        c = np.take_along_axis(o, slot, 2); nx = np.take_along_axis(h, c, 2)
        m = np.take_along_axis(so, slot[:, :, None, :], 3); low = nx; p = nx; n = 1
        while n < T:
            m = m + np.take_along_axis(m, p[:, :, None, :], 3); low = np.minimum(low, np.take_along_axis(low, p, 2)); p = np.take_along_axis(p, p, 2); n = 2 * n
        w = w + m
        r, g, v = np.nonzero((low == me) & (np.add.reduce((m > 0).astype(np.int64), axis=2) >= NEED))
        turn = np.zeros((N, 8, V), bool)
        for j in range(T):
            turn[r, g, v] = True; v = nx[r, g, v]
        r, g, v = np.nonzero(turn); u = nx[r, g, v]; e = c[r, g, v]
        o[r, g, slot[r, g, u]] = e; h[r, g, e] = v; s[r, g, :, e] = -s[r, g, :, e]
    return {"ys": s.reshape(N, 128, E).astype(np.float32).astype(BF), "yl": o.astype(np.float32), "yh": h.astype(np.float32), "yw": w.reshape(N, 128, V).astype(np.float32)}

@@ -1,0 +1,489 @@
+from concourse.bass import DstId, RemoteDMATransfer
+from concourse.mybir import AluOpType, ActivationFunctionType
+
+V, E, C = 1344, 4032, 84
+E1, E2 = E + V, E + 2 * V
+BF, F32, F16, I32, U16 = "bfloat16", "float32", "float16", "int32", "uint16"
+NCH = 3
+
+SCRATCH = {}
+for _d, _w, _names in [
+    (BF, E1, "SPW SNW YSW HW"), (F32, E1, "YHW"), (F32, E2, "EW"), (BF, E, "SO PR"), (F32, E, "YLW"),
+    (F32, V, "VROW X0 XF X WA WB"), (BF, V, "MS MA MB MD M32A M32B P1 PA PB POS NEG"), (F16, V, "TT EQ PD"),
+    (I32, 252, "LV"), (I32, 256, "LVN"), (I32, 592, "IN ILO IHI"), (BF, 592, "BLO BHI"),
+    (U16, 252, "LU1 LN1 LU2 LN2 LU3"), (U16, C * 9, "UL"), (F32, 252, "HDF L1F L2F BASE TIE OH CAND LMX"),
+    (F32, C * 16, "SM"), (I32, C * 5, "SI"), (F32, 144, "DM M0F"), (I32, 8, "PI"), (F32, 40, "COL"),
+    (F32, 128, "TB1 TB2 IDF"), (BF, 144, "MP MC MK MV"), (F16, 144, "M0H M15H M1H"), (F16, 128, "SH"),
+    (BF, 128, "BC INJ NINJ IDN IDE IDS"),
+]:
+    for _n in _names.split():
+        SCRATCH[_n] = ("sbuf", [128, _w], _d)
+for _n in ("R0", "R1", "R2", "L0", "L1", "L2", "L3", "L4"):
+    SCRATCH[_n] = ("psum", [128, 512], F32)
+
+SEMAPHORES = ["ev", "es", "et", "eg", "sent", "arrL", "arrS", "arrM", "arrN", "hL"] + \
+    ["h%d" % i for i in range(NCH)] + ["d%d" % i for i in range(56)]
+
+OP = AluOpType
+ACT = ActivationFunctionType
+
+
+def helper_of(src, dst, T, topo):
+    if topo.chip(src) == topo.chip(dst):
+        return None
+    for h in topo.cores_of(src):
+        if T.rank_of(h) is None and topo.die(h) != topo.die(src) and topo.may_write(h, dst):
+            return h
+    return None
+
+
+def bits(m):
+    return bin(m).count("1")
+
+
+def pieces():
+    w = E // NCH
+    return [("LV", "LVN", 0, 126, 252, "hL", "arrL")] + \
+        [("SPW", "SNW", i * w, i * w + w // 2, (i + 1) * w, "h%d" % i, "arrS") for i in range(NCH)]
+
+
+def helper_program(g, core, src, dst, T, topo):
+    rid, pid, _ = topo.addr(dst)
+    m = topo.mask(core, dst)
+    inc = bits(topo.mask(src, core) & ~topo.mask(src, dst))
+    n = 0
+    for _, land, a, b, c, hs, arr in pieces():
+        g.wait_ge(T.sem[hs], inc)
+        g.remote_dma(T[land][:, b:c], T[land][:, b:c], T.sem[arr], T.sem.sent, pid, rid, m)
+        n += bits(m)
+    g.wait_ge(T.sem.sent, n)
+
+
+def rank_program(g, core, T, topo):
+    n_rank = len(T.cores)
+    rank = T.rank_of(core)
+    if rank is None:
+        for r in range(n_rank):
+            src, dst = T.cores[r], T.cores[(r - 1) % n_rank]
+            if helper_of(src, dst, T, topo) == core:
+                helper_program(g, core, src, dst, T, topo)
+        return
+    dst = T.cores[(rank - 1) % n_rank]
+    src = T.cores[(rank + 1) % n_rank]
+    hout = helper_of(core, dst, T, topo)
+    hin = helper_of(src, core, T, topo)
+    in_direct = bits(topo.mask(src, core))
+    in_piece = in_direct + (bits(topo.mask(hin, core)) if hin is not None else 0)
+
+    Q = {"v": g.vector, "s": g.scalar, "t": g.tensor, "g": g, "y": g.sync}
+    total = {}
+    known = {q: {} for q in Q}
+    hist = {}
+    ndma = [0]
+
+    def wait(q, tok):
+        sem, val, clock = tok
+        if known[q].get(sem, 0) >= val:
+            return
+        Q[q].wait_ge(T.sem[sem], val)
+        known[q][sem] = val
+        for s, x in clock.items():
+            if known[q].get(s, 0) < x:
+                known[q][s] = x
+
+    def order(q, reads, writes, cont=False):
+        toks = []
+        for regs, wr in ((reads, False), (writes, True)):
+            for name, lo, hi in regs:
+                psum = name in SCRATCH and SCRATCH[name][0] == "psum"
+                for (l2, h2, w2, q2, tok) in hist.get(name, []):
+                    if psum:
+                        if q2 == q and (q == "t" and cont or not (wr or w2)):
+                            continue
+                        toks.append(tok)
+                    elif l2 < hi and lo < h2 and (wr or w2):
+                        toks.append(tok)
+        toks.sort(key=lambda t: -t[1])
+        for tok in toks:
+            wait(q, tok)
+
+    def note(q, reads, writes, tok):
+        for name, lo, hi in writes:
+            hist[name] = [x for x in hist.get(name, []) if not (lo <= x[0] and x[1] <= hi)] + [(lo, hi, True, q, tok)]
+        for name, lo, hi in reads:
+            hist.setdefault(name, []).append((lo, hi, False, q, tok))
+
+    def run(q, out, ins, call, cont=False):
+        w, r = out[1][:1], out[1][1:]
+        for x in ins:
+            r = r + x[1]
+        order(q, r, w, cont)
+        sem = "e" + q
+        total[sem] = total.get(sem, 0) + 1
+        call().then_inc(T.sem[sem], 1)
+        note(q, r, w, (sem, total[sem], dict(known[q])))
+
+    def A(name, lo=0, hi=None, step=None, part=None):
+        hi = SCRATCH[name][1][1] if hi is None else hi
+        cols = slice(lo, hi) if step is None else slice(lo, hi, step)
+        return (T[name][part if part is not None else slice(None), cols], [(name, lo, hi)])
+
+    def G(win, off):
+        return (win[0].indirect(off[0]), win[1] + off[1])
+
+    def sc(x):
+        return x if isinstance(x, tuple) else (x, [])
+
+    def copy(out, a):
+        run("v", out, [a], lambda: g.vector.tensor_copy(out[0], a[0]))
+
+    def tt(out, a, b, op):
+        run("v", out, [a, b], lambda: g.vector.tensor_tensor(out[0], a[0], b[0], op))
+
+    def ts(out, a, s1, op0, s2=None, op1=None):
+        s1, s2 = sc(s1), sc(s2)
+        ops = [op0] if op1 is None else [op0, op1]
+        run("v", out, [a, s1, s2], lambda: g.vector.tensor_scalar(out[0], a[0], s1[0], s2[0], *ops))
+
+    def memset(out, c):
+        run("v", out, [], lambda: g.vector.memset(out[0], c))
+
+    def act(out, a, func=ACT.Copy, **kw):
+        kw = {k: sc(x) for k, x in kw.items()}
+        run("s", out, [a] + list(kw.values()),
+            lambda: g.scalar.activation(out[0], a[0], func, **{k: x[0] for k, x in kw.items()}))
+
+    def iota(out, step, n, cm, flt=False):
+        kw = {"allow_small_or_imprecise_dtypes": True} if flt else {}
+        run("g", out, [], lambda: g.iota(out[0], [[step, n]], 0, cm, **kw))
+
+    def mm(out, pairs, start=True, stop=True):
+        def call():
+            ins = None
+            for i, (l, x) in enumerate(pairs):
+                ins = g.tensor.matmul(out[0], l[0], x[0], start and i == 0, stop and i == len(pairs) - 1)
+            return ins
+        run("t", out, [x for p in pairs for x in p], call, cont=not start)
+
+    def conv(bank, master, name, lo=0, start=True):
+        mm(A(bank, 0, C), [(A(master, 15 - i, 143 - i), A(name, lo + i, lo + V, 16)) for i in range(16)], start=start)
+
+    def dma(q, out, in_, **kw):
+        order(q, in_[1], out[1])
+        sem = "d%d" % ndma[0]
+        ndma[0] += 1
+        Q[q].dma_start(out[0], in_[0], **kw).then_inc(T.sem[sem], 16)
+        total[sem] = 16
+        note(q, in_[1], out[1], (sem, 16, dict(known[q])))
+
+    def H(name, ap):
+        return (ap, [(name, 0, 1)])
+
+    def arrival(name, lo, hi, sem, val):
+        total[sem] = val
+        note("r", [], [(name, lo, hi)], (sem, val, {}))
+
+    sent = [0]
+    rid, pid, _ = topo.addr(dst)
+    mdir = topo.mask(core, dst)
+
+    def send(land, src_ap, lo, hi, arr):
+        order("g", src_ap[1], [])
+        g.remote_dma(T[land][:, lo:hi], src_ap[0], T.sem[arr], T.sem.sent, pid, rid, mdir)
+        sent[0] += bits(mdir)
+
+    def send_piece(p):
+        name, land, a, b, c, hs, arr = p
+        if hout is None:
+            send(land, A(name, a, c), a, c, arr)
+            return
+        order("g", A(name, a, c)[1], [])
+        hrid, hpid, _ = topo.addr(hout)
+        mh = topo.mask(core, hout) & ~mdir
+        g.remote_dma_fused([
+            RemoteDMATransfer(dst_ids=[DstId(rid=rid, pnc=pid)], dma_engine_mask=mdir, remote_sem=T.sem[arr],
+                              src=T[name][:, a:b], dst=T[land][:, a:b]),
+            RemoteDMATransfer(dst_ids=[DstId(rid=hrid, pnc=hpid)], dma_engine_mask=mh, remote_sem=T.sem[hs],
+                              src=T[name][:, b:c], dst=T[land][:, b:c])], local_sem=T.sem.sent)
+        sent[0] += bits(mdir) + bits(mh)
+
+    arrival("LVN", 0, 252, "arrL", in_piece)
+    arrival("SNW", 0, E, "arrS", in_piece * NCH)
+    arrival("SNW", E, E1, "arrM", in_direct)
+    arrival("LN2", 0, 252, "arrN", in_direct)
+
+    def blk(name, k, w=C, a=0, b=None):
+        return A(name, k * w + a, k * w + (w if b is None else b))
+
+    def sm(i):
+        return blk("SM", i)
+
+    def si(i):
+        return blk("SI", i)
+
+    def ul(i, a=0, b=C):
+        return blk("UL", i, C, a, b)
+
+    def col(i, n=1):
+        return A("COL", i, i + n)
+
+    def ps(name):
+        return A(name, 0, C)
+
+    def HWW(lo, hi):
+        return (T.HW[:, lo:hi], [("HW", lo, hi)] + [("HWr%d" % r, lo, hi) for r in range(4)])
+
+    ROW = [slice(r, 128, 16) for r in range(4)]
+    RB = [("R0", 0, 512), ("R1", 512, 1024), ("R2", 1024, V)]
+    THIRDS = [(0, 28), (28, 56), (56, C)]
+    (VL, NV, DB, NC_, EQ32, U, CNT, REC, SU, NT, QQ, EE, FF, LOWN, LOW, ZZ) = range(16)
+    ENT, LOWU, TG1, TG2, PL = 0, 1, 2, 3, 4
+    (cR, c15, c1, cN, cE0, cE15, cWP, cWC, cN0, cWS, cT, cG, cG4, cG1, cM, cNWP, cBF) = range(17)
+    cB, cS, cBI = 20, 24, 28
+    KS = (1, 2, 0)
+    EQL, MUL, ADD, SUB = OP.is_equal, OP.mult, OP.add, OP.subtract
+
+    P = pieces()
+    dma("y", A("LV"), H("lv", T.lv[:]))
+    dma("s", A("IN", 0, 252), H("hd", T.hd[:]))
+    for p in P[1:]:
+        dma("y", A("SPW", p[2], p[4]), H("sp", T.sp[:, p[2]:p[4]]))
+    iota(A("PI", 0, 1), 1, 1, 1)
+    iota(A("DM"), 1, 144, -1, True)
+    iota(A("IN", 256, 508), 1, 252, 252)
+    iota(A("IN", 508, 592), 1, C, C)
+    send_piece(P[0])
+    iota(sm(VL), 16, C, 0, True)
+    for p in P[1:]:
+        send_piece(p)
+    iota(A("VROW"), 1, V, 0, True)
+    iota(A("EW", 0, E), 1, E, 0, True)
+
+    p0 = A("PI", 0, 1)
+    memset(A("HW"), 0.0)
+    ts(A("PI", 1, 2), p0, 15, OP.bitwise_and)
+    ts(A("PI", 2, 3), p0, 4, OP.arith_shift_right)
+    for j in range(4):
+        ts(A("PI", 4 + j, 5 + j), p0, j, OP.arith_shift_right, 1, OP.bitwise_and)
+    copy(A("LU1"), A("LV"))
+    copy(col(cR), A("PI", 1, 2))
+    copy(col(cG), A("PI", 2, 3))
+    copy(col(cB, 4), A("PI", 4, 8))
+    memset(A("IN", 252, 256), 0)
+    ts(col(cN0), col(cR), 0.5, OP.is_gt)
+    ts(col(cG4), col(cG), float(E), MUL)
+    ts(col(cG1), col(cG), float(V), MUL)
+    ts(col(cS, 4), col(cB, 4), -1.0, MUL, 1.0, ADD)
+    ts(col(c15), col(cR), -1.0, MUL, 15.0, ADD)
+    ts(col(cM), col(cN0), -2048.0, MUL)
+    tt(col(32, 2), col(cS, 2), col(cS + 2, 2), ADD)
+    ts(A("IN", 256, 508), A("IN", 256, 508), col(cG4), SUB)
+    ts(A("IN", 508, 592), A("IN", 508, 592), col(cG1), SUB)
+    ts(col(cBI, 4), col(cB, 4), 102048.0, MUL, col(cM), ADD)
+    ts(col(cBF), col(32), col(33), ADD, col(cM), MUL)
+    ts(A("ILO"), A("IN"), 63, OP.bitwise_and)
+    ts(A("IHI"), A("IN"), 6, OP.arith_shift_right)
+    copy(A("HDF"), A("IN", 0, 252))
+    copy(A("BLO"), A("ILO"))
+    copy(A("BHI"), A("IHI"))
+    for k in KS:
+        act(blk("SO", k, V), G(A("SPW", 0, E), blk("LU1", k)))
+    act(A("X0"), A("VROW"), ACT.Identity, bias=col(cBI), scale=col(cS))
+    act(A("XF"), A("VROW"), ACT.Identity, bias=col(cBF), scale=col(cN0))
+    order("y", [], [("HW", 0, E1)])
+    for r, name, a, b, lo, hi in ((0, "BLO", 0, 252, 0, E), (1, "BHI", 0, 252, 0, E), (2, "BLO", 256, 508, 0, E),
+                                  (3, "BHI", 256, 508, 0, E), (0, "BLO", 508, 592, E, E1), (1, "BHI", 508, 592, E, E1)):
+        dma("y", (T.HW[ROW[r], lo:hi], [("HWr%d" % r, lo, hi)]), A(name, a, b))
+    dma("y", A("YHW", 0, E, part=ROW[0]), A("HDF"))
+
+    ts(col(c1), col(cR), -1.0, MUL, 1.0, ADD)
+    ts(col(cN), col(cR), -1.0, MUL)
+    ts(col(cE0), col(cR), 0.0, EQL)
+    ts(col(cE15), col(cR), 15.0, EQL)
+    ts(col(cT), col(cR), 1.0, EQL, 64.0, MUL)
+    ts(col(34), col(cR), 2.0, EQL)
+    ts(col(35), col(cR), 3.0, EQL, 64.0, MUL)
+    memset(A("TIE", 0, 168), 8192.0)
+    memset(A("TIE", 168, 252), 0.0)
+    copy(A("L1F"), A("LV"))
+    tt(col(cWP), col(cT), col(cE0), ADD)
+    tt(col(cWC), col(34), col(35), ADD)
+    tt(col(cWS), col(cN0), col(cE15), SUB)
+    tt(A("BASE"), A("L1F"), A("TIE"), ADD)
+    ts(col(cNWP), col(cWP), -1.0, MUL)
+    for name, w in (("MK", 16384.0), ("MP", col(cWP)), ("MC", col(cWC)), ("MV", 8192.0), ("M0H", col(cE0)),
+                    ("M15H", col(cE15)), ("M1H", col(cN0)), ("M0F", col(cE0))):
+        ts(A(name), A("DM"), col(c15), EQL, w, MUL)
+    dm = A("DM", 0, 128)
+    for name, d, w in (("IDF", 0.0, 1.0), ("INJ", col(c1), col(cWP)), ("NINJ", col(c1), col(cNWP)),
+                       ("SH", 1.0, col(cWS)), ("IDN", 0.0, -8192.0), ("IDE", 0.0, -2.0 ** -20), ("IDS", 0.0, 2.0 ** -6)):
+        ts(A(name), dm, d, EQL, w, MUL)
+    ts(A("TB1"), dm, col(cN), OP.is_ge, col(cWP), MUL)
+    ts(A("TB2"), dm, col(c15), OP.is_le)
+    ts(sm(VL), sm(VL), col(cR), ADD)
+    memset(A("NEG"), -1.0)
+    tt(A("BC"), A("TB1"), A("TB2"), MUL)
+    ts(sm(NV), sm(VL), -1.0, MUL, -float(E), ADD)
+    copy(A("LN1"), A("LVN", 0, 252))
+
+    def scatter_heads(tg, a, b):
+        copy(G(A("YHW"), ul(tg, a, b)), A("VROW", 16 * a, 16 * b))
+
+    def mirror(name, a, b):
+        dma("y", A("MD", 16 * a, 16 * b), A(name, 16 * a, 16 * b))
+
+    def madd(out, win, j, more=True):
+        for a, b in THIRDS:
+            tt(A(out, 16 * a, 16 * b), G(A(win), ul(j, a, b)), A("MD", 16 * a, 16 * b), ADD)
+            if more:
+                mirror(out, a, b)
+
+    for rnd in range(2):
+        last = rnd == 1
+        wid = E1 if last else E
+        ln, lf = ("LN2", "L2F") if last else ("LN1", "L1F")
+        m32 = "M32B" if last else "M32A"
+        KB = {1: "L0", 2: "L1", 0: "L2"}
+
+        for k in KS:
+            mm(ps(KB[k]), [(A("IDF"), blk("BASE", k))], stop=False)
+        for k in KS:
+            tt(blk("PR", k, V), G(A("SNW", 0, wid), blk(ln, k)), blk("SO", k, V), MUL)
+            conv(KB[k], "MK", "PR", k * V, start=False)
+            if k == 2:
+                copy(si(0), ps("L0"))
+        if not last:
+            order("y", [("SNW", 0, E)], [])
+            dma("y", A("YSW", 0, E), H("sp", T.sp[:]))
+        tt(si(1), ps("L1"), si(0), OP.max)
+        ts(si(2), si(1), -8193, OP.bitwise_and)
+        tt(si(3), ps("L2"), si(2), OP.max)
+        ts(si(4), si(3), 8191, OP.bitwise_and)
+        copy(ul(ENT), si(4))
+
+        act(A("P1"), G(HWW(0, wid), ul(ENT)))
+        for a, b in THIRDS:
+            (act if last else copy)(A("MS", 16 * a, 16 * b), G(A("SPW", 0, wid), ul(ENT, a, b)))
+            mirror("MS", a, b)
+        if last:
+            scatter_heads(TG1, 0, C // 2)
+        conv("L3", "MP", "P1")
+        for b, lo, hi in RB:
+            mm(A(b, 0, hi - lo), [(A("BC"), A("P1", lo, hi))])
+        for k in range(3):
+            tt(blk("OH", k), blk(lf, k), si(4), EQL)
+        ts(sm(DB), sm(VL), wid + 0.25, ADD)
+        copy(ul(PL), ps("L3"))
+        act(A("PA"), G(A("P1"), ul(PL)))
+        for b, lo, hi in RB:
+            tt(A("WA", lo, hi), A(b, 0, hi - lo), A("X0", lo, hi), OP.min)
+        conv("L4", "MP", "PA")
+        if last:
+            conv("L0", "MC", "P1")
+            scatter_heads(TG1, C // 2, C)
+        madd("MA", "MS", PL)
+        if not last:
+            ts(sm(NC_), si(4), -1.0, MUL)
+            for r in (2, 3):
+                dma("y", (T.HW[ROW[r], E:E1], [("HWr%d" % r, E, E1)]), A("P1", part=ROW[r]))
+        for b, lo, hi in RB:
+            mm(A(b, 0, hi - lo), [(A("NINJ"), (T.HW[:, E + lo:E + hi], HWW(E, E1)[1]))], stop=False)
+
+        pw, ww, mw, lb = ["PA", "PB"], ["WA", "WB"], ["MA", "MB"], ["L4", "L3"]
+        for j in (1, 2, 3):
+            a, b = (j - 1) % 2, j % 2
+            act(A("X"), A(ww[a]), ACT.Identity, bias=col(cBI + j), scale=col(cS + j))
+            copy(ul(PL + j), ps(lb[a]))
+            act(A(pw[b]), G(A(pw[a]), ul(PL + j)))
+            conv(lb[b], "MP", pw[b])
+            tt(A(ww[b]), G(A(ww[a]), ul(PL + j)), A("X"), OP.min)
+            madd(mw[b], mw[a], PL + j)
+            if j == 1 and last:
+                ts(sm(NC_), ps("L0"), -1.0, MUL)
+        for b, lo, hi in RB:
+            mm(A(b, 0, hi - lo), [(A("INJ"), A("PB", lo, hi))], start=False, stop=False)
+        conv("L1", "M0F", "WB")
+
+        copy(ul(PL + 4), ps("L3"))
+        act(A("PA"), G(A("PB"), ul(PL + 4)))
+        if last:
+            act(A("EW", E1, E2), G(A("EW", 0, E1), ul(ENT)))
+        else:
+            act(A("SPW", E, E1), A("MS"), scale=-1.0)
+            send("SNW", A("SPW", E, E1), E, E1, "arrM")
+        tt(A("TT"), G(A("WB"), ul(PL + 4)), A("XF"), SUB)
+        conv("L0", "M0H", "TT")
+        for b, lo, hi in RB:
+            mm(A(b, 0, hi - lo), [(A("SH"), A("TT", lo, hi))], start=False)
+        conv("L2", "M15H", "TT")
+        conv("L3", "MP", "PA")
+        madd(m32, "MB", PL + 4, False)
+        copy(sm(LOWN), ps("L1"))
+        tt(sm(LOW), ps("L0"), sm(LOWN), OP.min)
+        copy(ul(LOWU), sm(LOW))
+        act(A("POS"), G(A(m32), ul(LOWU)), ACT.Sign, bias=-0.5)
+        if not last:
+            act(A("EW", E, E1), G(A("EW", 0, E), ul(ENT)))
+        ts(A("EQ"), A("TT"), 0.0, EQL)
+        mm(ps("L4"), [(A("IDE"), A("NEG", 0, C))], stop=False)
+        mm(ps("L0"), [(A("IDS"), A("NEG", 0, C))], stop=False)
+        conv("L4", "M1H", "EQ", start=False)
+        for b, lo, hi in RB:
+            tt(A("PD", lo, hi), A(b, 0, hi - lo), A("EQ", lo, hi), MUL)
+        mm(ps("L1"), [(A("IDN"), A("NEG", 0, C))], stop=False)
+        conv("L0", "M1H", "PD", start=False)
+        conv("L1", "MV", "POS", start=False)
+        if last:
+            dma("g", H("yw", T.yw[:]), A(m32), accum_op=ADD)
+        tt(sm(EQ32), ps("L3"), sm(VL), EQL)
+        tt(sm(CNT), ps("L4"), sm(EQ32), ADD)
+        tt(sm(U), ps("L2"), sm(EQ32), MUL)
+        run("v", sm(REC), [sm(CNT)], lambda: g.vector.reciprocal(sm(REC)[0], sm(CNT)[0]))
+        tt(sm(SU), ps("L0"), sm(U), ADD)
+        tg = TG2 if last else TG1
+        lu = "LU3" if last else "LU2"
+
+        def targets(step):
+            if step == 1:
+                tt(sm(ZZ), sm(FF), sm(NC_), OP.min)
+            elif step == 2:
+                tt(sm(NT), sm(ZZ), sm(NV), OP.max)
+            else:
+                ts(ul(tg), sm(NT), -1.0, MUL)
+
+        tt(sm(QQ), sm(SU), sm(REC), MUL)
+        tt(sm(EE), sm(QQ), sm(DB), ADD)
+        tt(sm(FF), ps("L1"), sm(EE), OP.min)
+        if last:
+            targets(1)
+        for k in range(3):
+            tt(blk("CAND", k), blk("OH", k), sm(FF), MUL)
+        if last:
+            targets(2)
+        tt(A("LMX"), A("CAND"), A(lf), OP.max)
+        if last:
+            targets(3)
+        copy(A(lu), A("LMX"))
+        if not last:
+            send("LN2", A("LU2"), 0, 252, "arrN")
+            for k in KS:
+                act(blk("SO", k, V), G(A("SPW"), blk("LU2", k)))
+            copy(A("L2F"), A("LU2"))
+            targets(1)
+            tt(A("BASE"), A("L2F"), A("TIE"), ADD)
+            targets(2)
+            targets(3)
+            dma("g", H("yw", T.yw[:]), A(m32))
+            copy(G(A("YSW"), ul(tg)), A("SPW", E, E1))
+        else:
+            tt(G(A("YSW"), ul(tg)), A("MS"), A("NEG"), MUL)
+            dma("y", H("ys", T.ys[:]), A("YSW", 0, E))
+            for k in range(3):
+                act(blk("YLW", k, V), G(A("EW"), blk("LU3", k)))
+            dma("s", H("yl", T.yl[:]), A("YLW", part=ROW[0]))
+            scatter_heads(tg, 0, C)
+            dma("y", H("yh", T.yh[:]), A("YHW", 0, E, part=ROW[0]))
+
+    total["sent"] = sent[0]
+    for s in sorted(total):
+        wait("g", (s, total[s], {}))

@@ -4,15 +4,16 @@ from concourse.mybir import AluOpType, ActivationFunctionType
 V, E, C = 1344, 4032, 84
 E1, E2 = E + V, E + 2 * V
 BF, F32, F16, I32, U16 = "bfloat16", "float32", "float16", "int32", "uint16"
-NCH = 3
+CUT = [0, 1728, 3456, E]
+NCH = len(CUT) - 1
 
 SCRATCH = {}
 for _d, _w, _names in [
     (BF, E1, "SPW SNW YSW HW"), (F32, E1, "YHW"), (F32, E2, "EW"), (BF, E, "SO PR"), (F32, E, "YLW"),
-    (F32, V, "VROW X0 XF X WA WB"), (BF, V, "MS MA MB MD M32A M32B P1 PA PB POS NEG"), (F16, V, "TT EQ PD"),
+    (F32, V, "VROW V64 X0 XF X WA WB"), (BF, V, "MS MA MB MD M32A M32B P1 PA PB POS NEG"), (F16, V, "TT EQ PD"),
     (I32, 252, "LV"), (I32, 256, "LVN"), (I32, 592, "IN ILO IHI"), (BF, 592, "BLO BHI"),
-    (U16, 252, "LU1 LN1 LU2 LN2 LU3"), (U16, C * 9, "UL"), (F32, 252, "HDF L1F L2F BASE TIE OH CAND LMX"),
-    (F32, C * 16, "SM"), (I32, C * 5, "SI"), (F32, 144, "DM M0F"), (I32, 8, "PI"), (F32, 40, "COL"),
+    (U16, 252, "LU1 LN1 LU2 LN2 LU3"), (U16, C * 9, "UL"), (F32, 252, "HDF HR1 L1F L2F OH CAND LMX"),
+    (F32, C * 17, "SM"), (I32, C * 5, "SI"), (F32, 144, "DM M0F"), (I32, 8, "PI"), (F32, 40, "COL"),
     (F32, 128, "TB1 TB2 IDF"), (BF, 144, "MP MC MK MV"), (F16, 144, "M0H M15H M1H"), (F16, 128, "SH"),
     (BF, 128, "BC INJ NINJ IDN IDE IDS"),
 ]:
@@ -22,7 +23,7 @@ for _n in ("R0", "R1", "R2", "L0", "L1", "L2", "L3", "L4"):
     SCRATCH[_n] = ("psum", [128, 512], F32)
 
 SEMAPHORES = ["ev", "es", "et", "eg", "sent", "arrL", "arrS", "arrM", "arrN", "hL"] + \
-    ["h%d" % i for i in range(NCH)] + ["d%d" % i for i in range(56)]
+    ["h%d" % i for i in range(NCH - 1)] + ["d%d" % i for i in range(60)]
 
 OP = AluOpType
 ACT = ActivationFunctionType
@@ -42,9 +43,8 @@ def bits(m):
 
 
 def pieces():
-    w = E // NCH
     return [("LV", "LVN", 0, 126, 252, "hL", "arrL")] + \
-        [("SPW", "SNW", i * w, i * w + w // 2, (i + 1) * w, "h%d" % i, "arrS") for i in range(NCH)]
+        [("SPW", "SNW", CUT[i], (CUT[i] + CUT[i + 1]) // 2, CUT[i + 1], "h%d" % i, "arrS") for i in range(NCH)]
 
 
 def helper_program(g, core, src, dst, T, topo):
@@ -52,7 +52,7 @@ def helper_program(g, core, src, dst, T, topo):
     m = topo.mask(core, dst)
     inc = bits(topo.mask(src, core) & ~topo.mask(src, dst))
     n = 0
-    for _, land, a, b, c, hs, arr in pieces():
+    for _, land, a, b, c, hs, arr in pieces()[:-1]:
         g.wait_ge(T.sem[hs], inc)
         g.remote_dma(T[land][:, b:c], T[land][:, b:c], T.sem[arr], T.sem.sent, pid, rid, m)
         n += bits(m)
@@ -194,7 +194,7 @@ def rank_program(g, core, T, topo):
 
     def send_piece(p):
         name, land, a, b, c, hs, arr = p
-        if hout is None:
+        if hout is None or c == E:
             send(land, A(name, a, c), a, c, arr)
             return
         order("g", A(name, a, c)[1], [])
@@ -208,7 +208,7 @@ def rank_program(g, core, T, topo):
         sent[0] += bits(mdir) + bits(mh)
 
     arrival("LVN", 0, 252, "arrL", in_piece)
-    arrival("SNW", 0, E, "arrS", in_piece * NCH)
+    arrival("SNW", 0, E, "arrS", in_piece * (NCH - 1) + in_direct)
     arrival("SNW", E, E1, "arrM", in_direct)
     arrival("LN2", 0, 252, "arrN", in_direct)
 
@@ -236,7 +236,7 @@ def rank_program(g, core, T, topo):
     ROW = [slice(r, 128, 16) for r in range(4)]
     RB = [("R0", 0, 512), ("R1", 512, 1024), ("R2", 1024, V)]
     THIRDS = [(0, 28), (28, 56), (56, C)]
-    (VL, NV, DB, NC_, EQ32, U, CNT, REC, SU, NT, QQ, EE, FF, LOWN, LOW, ZZ) = range(16)
+    (VL, NV, DB, NC_, EQ32, U, CNT, REC, SU, NT, QQ, EE, FF, LOWN, LOW, ZZ, DB2) = range(17)
     ENT, LOWU, TG1, TG2, PL = 0, 1, 2, 3, 4
     (cR, c15, c1, cN, cE0, cE15, cWP, cWC, cN0, cWS, cT, cG, cG4, cG1, cM, cNWP, cBF) = range(17)
     cB, cS, cBI = 20, 24, 28
@@ -283,13 +283,14 @@ def rank_program(g, core, T, topo):
     ts(col(cBF), col(32), col(33), ADD, col(cM), MUL)
     ts(A("ILO"), A("IN"), 63, OP.bitwise_and)
     ts(A("IHI"), A("IN"), 6, OP.arith_shift_right)
-    copy(A("HDF"), A("IN", 0, 252))
+    ts(A("HDF"), A("IN", 0, 252), 64.0, ADD)
     copy(A("BLO"), A("ILO"))
     copy(A("BHI"), A("IHI"))
     for k in KS:
         act(blk("SO", k, V), G(A("SPW", 0, E), blk("LU1", k)))
     act(A("X0"), A("VROW"), ACT.Identity, bias=col(cBI), scale=col(cS))
     act(A("XF"), A("VROW"), ACT.Identity, bias=col(cBF), scale=col(cN0))
+    act(A("V64"), A("VROW"), ACT.Identity, bias=64.0)
     order("y", [], [("HW", 0, E1)])
     for r, name, a, b, lo, hi in ((0, "BLO", 0, 252, 0, E), (1, "BHI", 0, 252, 0, E), (2, "BLO", 256, 508, 0, E),
                                   (3, "BHI", 256, 508, 0, E), (0, "BLO", 508, 592, E, E1), (1, "BHI", 508, 592, E, E1)):
@@ -303,13 +304,10 @@ def rank_program(g, core, T, topo):
     ts(col(cT), col(cR), 1.0, EQL, 64.0, MUL)
     ts(col(34), col(cR), 2.0, EQL)
     ts(col(35), col(cR), 3.0, EQL, 64.0, MUL)
-    memset(A("TIE", 0, 168), 8192.0)
-    memset(A("TIE", 168, 252), 0.0)
     copy(A("L1F"), A("LV"))
     tt(col(cWP), col(cT), col(cE0), ADD)
     tt(col(cWC), col(34), col(35), ADD)
     tt(col(cWS), col(cN0), col(cE15), SUB)
-    tt(A("BASE"), A("L1F"), A("TIE"), ADD)
     ts(col(cNWP), col(cWP), -1.0, MUL)
     for name, w in (("MK", 16384.0), ("MP", col(cWP)), ("MC", col(cWC)), ("MV", 8192.0), ("M0H", col(cE0)),
                     ("M15H", col(cE15)), ("M1H", col(cN0)), ("M0F", col(cE0))):
@@ -324,10 +322,12 @@ def rank_program(g, core, T, topo):
     memset(A("NEG"), -1.0)
     tt(A("BC"), A("TB1"), A("TB2"), MUL)
     ts(sm(NV), sm(VL), -1.0, MUL, -float(E), ADD)
+    ts(sm(DB), sm(VL), E + 0.25, ADD)
+    ts(sm(DB2), sm(VL), E1 + 0.25, ADD)
     copy(A("LN1"), A("LVN", 0, 252))
 
-    def scatter_heads(tg, a, b):
-        copy(G(A("YHW"), ul(tg, a, b)), A("VROW", 16 * a, 16 * b))
+    def scatter_spins(a, b):
+        copy(G(A("YSW"), ul(TG1, a, b)), A("SPW", E + 16 * a, E + 16 * b))
 
     def mirror(name, a, b):
         dma("y", A("MD", 16 * a, 16 * b), A(name, 16 * a, 16 * b))
@@ -346,7 +346,7 @@ def rank_program(g, core, T, topo):
         KB = {1: "L0", 2: "L1", 0: "L2"}
 
         for k in KS:
-            mm(ps(KB[k]), [(A("IDF"), blk("BASE", k))], stop=False)
+            mm(ps(KB[k]), [(A("IDF"), blk(lf, k))] + ([(A("IDN"), A("NEG", 0, C))] if k != 2 else []), stop=False)
         for k in KS:
             tt(blk("PR", k, V), G(A("SNW", 0, wid), blk(ln, k)), blk("SO", k, V), MUL)
             conv(KB[k], "MK", "PR", k * V, start=False)
@@ -363,16 +363,15 @@ def rank_program(g, core, T, topo):
 
         act(A("P1"), G(HWW(0, wid), ul(ENT)))
         for a, b in THIRDS:
-            (act if last else copy)(A("MS", 16 * a, 16 * b), G(A("SPW", 0, wid), ul(ENT, a, b)))
+            (act if b == C or last and a else copy)(A("MS", 16 * a, 16 * b), G(A("SPW", 0, wid), ul(ENT, a, b)))
             mirror("MS", a, b)
         if last:
-            scatter_heads(TG1, 0, C // 2)
+            scatter_spins(C // 2, C)
         conv("L3", "MP", "P1")
         for b, lo, hi in RB:
             mm(A(b, 0, hi - lo), [(A("BC"), A("P1", lo, hi))])
         for k in range(3):
             tt(blk("OH", k), blk(lf, k), si(4), EQL)
-        ts(sm(DB), sm(VL), wid + 0.25, ADD)
         copy(ul(PL), ps("L3"))
         act(A("PA"), G(A("P1"), ul(PL)))
         for b, lo, hi in RB:
@@ -380,12 +379,9 @@ def rank_program(g, core, T, topo):
         conv("L4", "MP", "PA")
         if last:
             conv("L0", "MC", "P1")
-            scatter_heads(TG1, C // 2, C)
         madd("MA", "MS", PL)
         if not last:
             ts(sm(NC_), si(4), -1.0, MUL)
-            for r in (2, 3):
-                dma("y", (T.HW[ROW[r], E:E1], [("HWr%d" % r, E, E1)]), A("P1", part=ROW[r]))
         for b, lo, hi in RB:
             mm(A(b, 0, hi - lo), [(A("NINJ"), (T.HW[:, E + lo:E + hi], HWW(E, E1)[1]))], stop=False)
 
@@ -398,8 +394,8 @@ def rank_program(g, core, T, topo):
             conv(lb[b], "MP", pw[b])
             tt(A(ww[b]), G(A(ww[a]), ul(PL + j)), A("X"), OP.min)
             madd(mw[b], mw[a], PL + j)
-            if j == 1 and last:
-                ts(sm(NC_), ps("L0"), -1.0, MUL)
+            if j == 3 and last:
+                act(sm(NC_), ps("L0"), scale=-1.0)
         for b, lo, hi in RB:
             mm(A(b, 0, hi - lo), [(A("INJ"), A("PB", lo, hi))], start=False, stop=False)
         conv("L1", "M0F", "WB")
@@ -411,6 +407,9 @@ def rank_program(g, core, T, topo):
         else:
             act(A("SPW", E, E1), A("MS"), scale=-1.0)
             send("SNW", A("SPW", E, E1), E, E1, "arrM")
+            for r in (2, 3):
+                dma("y", (T.HW[ROW[r], E:E1], [("HWr%d" % r, E, E1)]), A("P1", part=ROW[r]))
+        act(sm(LOWN), ps("L1"))
         tt(A("TT"), G(A("WB"), ul(PL + 4)), A("XF"), SUB)
         conv("L0", "M0H", "TT")
         for b, lo, hi in RB:
@@ -418,7 +417,6 @@ def rank_program(g, core, T, topo):
         conv("L2", "M15H", "TT")
         conv("L3", "MP", "PA")
         madd(m32, "MB", PL + 4, False)
-        copy(sm(LOWN), ps("L1"))
         tt(sm(LOW), ps("L0"), sm(LOWN), OP.min)
         copy(ul(LOWU), sm(LOW))
         act(A("POS"), G(A(m32), ul(LOWU)), ACT.Sign, bias=-0.5)
@@ -452,37 +450,37 @@ def rank_program(g, core, T, topo):
                 ts(ul(tg), sm(NT), -1.0, MUL)
 
         tt(sm(QQ), sm(SU), sm(REC), MUL)
-        tt(sm(EE), sm(QQ), sm(DB), ADD)
+        tt(sm(EE), sm(QQ), sm(DB2 if last else DB), ADD)
         tt(sm(FF), ps("L1"), sm(EE), OP.min)
         if last:
-            targets(1)
+            for step in (1, 2, 3):
+                targets(step)
+            act(G(A("YHW"), ul(tg)), A("V64"), ACT.Silu)
+            dma("s", A("HDF"), A("YHW", 0, E, part=ROW[0]))
         for k in range(3):
             tt(blk("CAND", k), blk("OH", k), sm(FF), MUL)
-        if last:
-            targets(2)
         tt(A("LMX"), A("CAND"), A(lf), OP.max)
-        if last:
-            targets(3)
         copy(A(lu), A("LMX"))
         if not last:
             send("LN2", A("LU2"), 0, 252, "arrN")
             for k in KS:
                 act(blk("SO", k, V), G(A("SPW"), blk("LU2", k)))
-            copy(A("L2F"), A("LU2"))
             targets(1)
-            tt(A("BASE"), A("L2F"), A("TIE"), ADD)
+            copy(A("L2F"), A("LU2"))
             targets(2)
             targets(3)
             dma("g", H("yw", T.yw[:]), A(m32))
-            copy(G(A("YSW"), ul(tg)), A("SPW", E, E1))
+            scatter_spins(0, C // 2)
+            act(G(A("YHW"), ul(tg)), A("V64"), ACT.Silu)
         else:
             tt(G(A("YSW"), ul(tg)), A("MS"), A("NEG"), MUL)
             dma("y", H("ys", T.ys[:]), A("YSW", 0, E))
-            for k in range(3):
-                act(blk("YLW", k, V), G(A("EW"), blk("LU3", k)))
-            dma("s", H("yl", T.yl[:]), A("YLW", part=ROW[0]))
-            scatter_heads(tg, 0, C)
-            dma("y", H("yh", T.yh[:]), A("YHW", 0, E, part=ROW[0]))
+            for f, q, a, b in ((act, "s", 0, 168), (copy, "y", 168, 252)):
+                f(A("YLW", 16 * a, 16 * b), G(A("EW"), A("LU3", a, b)))
+                dma(q, H("yl%d" % a, T.yl[:, 16 * a:16 * b]), A("YLW", 16 * a, 16 * b, part=ROW[0]))
+            copy(A("ILO", 0, 252), A("HDF"))
+            ts(A("HR1"), A("ILO", 0, 252), -64.0, ADD)
+            dma("y", H("yh", T.yh[:]), A("HR1"))
 
     total["sent"] = sent[0]
     for s in sorted(total):

@@ -6,20 +6,30 @@ E1, E2 = E + V, E + 2 * V
 BF, F32, F16, I32, U16 = "bfloat16", "float32", "float16", "int32", "uint16"
 CUT = [0, 1728, 3456, E]
 NCH = len(CUT) - 1
+UP = 16384.0
+OPT = dict(yl=140, yh=224, sc=(0, 48, 70, 76, 84), hs=(0, 72, 84), p1=42, lu_first=True, help=5)
+
+WALK = ("DG P1 Mv0 Mv1 Mv2:0 Ms2:1 NV c0 BC ENS MC:1 neg:0 sc1:1 l0 h0 sc2:1 w00 w01 w02 x1 c1 m00 m01 l1 h1 m02 "
+        "w1 D c2 x2 m10 m11 l2 app h2 NC:1 m12 w2 c3 PEN x3 NBC m20 m21 l3 h3 LF:1 m22 c4 "
+        "w3 x4 m30 m31 l4 h4 m32 g2 snd:0 INJ "
+        "w40 SH_0 w41 SH_1 w42 I32_0 IP_0 q2 k2 low I32_1 IP_1 I32_2 IP_2 SH_2 m40 m41 min POS hs1:1 LF:0 NC:0 "
+        "eq0 eq1 EM_0 EM_1 eq2 EM_2 y0 y1 y2 cv VV HD:0 pen cy")
+ORDER = [" ".join(x.split(":")[0] for x in WALK.split() if x.split(":")[-1] != str(1 - r)) for r in range(2)]
+AFTER = "sc0 hs0"
 
 SCRATCH = {}
 for _d, _w, _names in [
     (BF, E1, "SPW SNW YSW HW"), (F32, E1, "YHW"), (F32, E2, "EW"), (BF, E, "SO PR"), (F32, E, "YLW"),
-    (F32, V, "VROW V64 X0 XF X WA WB"), (BF, V, "MS MA MB MD M32A M32B P1 PA PB POS NEG"), (F16, V, "TT EQ PD"),
-    (I32, 252, "LV"), (I32, 256, "LVN"), (I32, 592, "IN ILO IHI"), (BF, 592, "BLO BHI"),
-    (U16, 252, "LU1 LN1 LU2 LN2 LU3"), (U16, C * 9, "UL"), (F32, 252, "HDF HR1 L1F L2F OH CAND LMX"),
-    (F32, C * 17, "SM"), (I32, C * 5, "SI"), (F32, 144, "DM M0F"), (I32, 8, "PI"), (F32, 40, "COL"),
-    (F32, 128, "TB1 TB2 IDF"), (BF, 144, "MP MC MK MV"), (F16, 144, "M0H M15H M1H"), (F16, 128, "SH"),
-    (BF, 128, "BC INJ NINJ IDN IDE IDS"),
+    (F32, V, "VROW X0 X WA WB"), (BF, V, "MS MA MB MD M32A M32B P1 PA PB POS NEG EQ"), (F16, V, "TT PD"),
+    (I32, 252, "LV LVN"), (I32, 588, "IN ILO IHI"), (BF, 588, "BLO BHI"),
+    (U16, 252, "LU1 LN1 LU2 LN2 LU3"), (U16, C * 9, "UL"), (F32, 252, "HDF HR1 L1S L2S LFL LMX"), (BF, 252, "PEN"),
+    (F32, C * 12, "SM"), (I32, C * 5, "SI"), (F32, 144, "DM M1"), (I32, 8, "PI"),
+    (F32, 32, "COL"), (F32, 16, "J LT EQJ DJ"), (F32, 128, "TB1 TB2 TB3 IDF IDM"), (BF, 144, "MP MC MK"),
+    (F16, 144, "M0H MH"), (F16, 128, "SH IP"), (BF, 128, "EM BC NBC INJ I32 DG IB IBM IDN IDE"), (BF, 448, "AB"),
 ]:
     for _n in _names.split():
         SCRATCH[_n] = ("sbuf", [128, _w], _d)
-for _n in ("R0", "R1", "R2", "L0", "L1", "L2", "L3", "L4"):
+for _n in ("R0", "R1", "R2", "Q0", "Q1", "Q2", "L0", "L1"):
     SCRATCH[_n] = ("psum", [128, 512], F32)
 
 SEMAPHORES = ["ev", "es", "et", "eg", "sent", "arrL", "arrS", "arrM", "arrN", "hL"] + \
@@ -153,9 +163,12 @@ def rank_program(g, core, T, topo):
         run("s", out, [a] + list(kw.values()),
             lambda: g.scalar.activation(out[0], a[0], func, **{k: x[0] for k, x in kw.items()}))
 
-    def iota(out, step, n, cm, flt=False):
+    def lin(out, a, scale=1.0, bias=0.0):
+        act(out, a, ACT.Identity, scale=scale, bias=bias)
+
+    def iota(out, pattern, cm, flt=False, base=0):
         kw = {"allow_small_or_imprecise_dtypes": True} if flt else {}
-        run("g", out, [], lambda: g.iota(out[0], [[step, n]], 0, cm, **kw))
+        run("g", out, [], lambda: g.iota(out[0], pattern, base, cm, **kw))
 
     def mm(out, pairs, start=True, stop=True):
         def call():
@@ -165,8 +178,9 @@ def rank_program(g, core, T, topo):
             return ins
         run("t", out, [x for p in pairs for x in p], call, cont=not start)
 
-    def conv(bank, master, name, lo=0, start=True):
-        mm(A(bank, 0, C), [(A(master, 15 - i, 143 - i), A(name, lo + i, lo + V, 16)) for i in range(16)], start=start)
+    def conv(bank, master, name, lo=0, start=True, stop=True, at=0):
+        mm(A(bank, at, at + C), [(A(master, 15 - i, 143 - i), A(name, lo + i, lo + V, 16)) for i in range(16)],
+           start=start, stop=stop)
 
     def dma(q, out, in_, **kw):
         order(q, in_[1], out[1])
@@ -215,272 +229,331 @@ def rank_program(g, core, T, topo):
     def blk(name, k, w=C, a=0, b=None):
         return A(name, k * w + a, k * w + (w if b is None else b))
 
-    def sm(i):
-        return blk("SM", i)
+    def sm(i, n=1):
+        return A("SM", i * C, (i + n) * C)
 
-    def si(i):
-        return blk("SI", i)
+    def si(i, n=1):
+        return A("SI", i * C, (i + n) * C)
 
     def ul(i, a=0, b=C):
         return blk("UL", i, C, a, b)
 
-    def col(i, n=1):
-        return A("COL", i, i + n)
+    def col(i, n=1, name="COL"):
+        return A(name, i, i + n)
 
-    def ps(name):
-        return A(name, 0, C)
+    def ps(name, a=0, b=1):
+        return A(name, a * C, b * C)
+
+    def part(name, a, b, lo=0):
+        return A(name, lo + 16 * a, lo + 16 * b)
 
     def HWW(lo, hi):
         return (T.HW[:, lo:hi], [("HW", lo, hi)] + [("HWr%d" % r, lo, hi) for r in range(4)])
 
+    def row(r, lo, hi):
+        return (T.HW[ROW[r], lo:hi], [("HWr%d" % r, lo, hi)])
+
     ROW = [slice(r, 128, 16) for r in range(4)]
-    RB = [("R0", 0, 512), ("R1", 512, 1024), ("R2", 1024, V)]
     THIRDS = [(0, 28), (28, 56), (56, C)]
-    (VL, NV, DB, NC_, EQ32, U, CNT, REC, SU, NT, QQ, EE, FF, LOWN, LOW, ZZ, DB2) = range(17)
+    (VL, NV, NC_, ENS, NT, EE, FF, ZZ, LOWN, LOW, EQ32, U) = range(12)
     ENT, LOWU, TG1, TG2, PL = 0, 1, 2, 3, 4
-    (cR, c15, c1, cN, cE0, cE15, cWP, cWC, cN0, cWS, cT, cG, cG4, cG1, cM, cNWP, cBF) = range(17)
-    cB, cS, cBI = 20, 24, 28
+    (cR, cG, cG4, cG1, cSEL, cW23, cOFF, cBIG, cDG, cSH, cM, cT, cU, cN) = range(14)
+    BIG = 100000.0
+    cB, cS, cBI = 16, 20, 24
     KS = (1, 2, 0)
-    EQL, MUL, ADD, SUB = OP.is_equal, OP.mult, OP.add, OP.subtract
+    EQL, MUL, ADD, SUB, MIN, MAX = OP.is_equal, OP.mult, OP.add, OP.subtract, OP.min, OP.max
 
     P = pieces()
     dma("y", A("LV"), H("lv", T.lv[:]))
     dma("s", A("IN", 0, 252), H("hd", T.hd[:]))
     for p in P[1:]:
         dma("y", A("SPW", p[2], p[4]), H("sp", T.sp[:, p[2]:p[4]]))
-    iota(A("PI", 0, 1), 1, 1, 1)
-    iota(A("DM"), 1, 144, -1, True)
-    iota(A("IN", 256, 508), 1, 252, 252)
-    iota(A("IN", 508, 592), 1, C, C)
-    send_piece(P[0])
-    iota(sm(VL), 16, C, 0, True)
-    for p in P[1:]:
+    iota(A("PI", 0, 1), [[1, 1]], 1)
+    iota(A("J"), [[1, 16]], 0, True)
+    iota(A("DM"), [[1, 144]], -1, True)
+    iota(A("IN", 252, 504), [[1, 252]], 252)
+    iota(A("IN", 504, 588), [[1, C]], C)
+    iota(sm(VL), [[16, C]], 0, True)
+    for p in P:
         send_piece(p)
-    iota(A("VROW"), 1, V, 0, True)
-    iota(A("EW", 0, E), 1, E, 0, True)
+    iota(A("VROW"), [[1, V]], 0, True, 64)
+    iota(A("EW"), [[1, E2]], 0, True)
 
-    p0 = A("PI", 0, 1)
-    memset(A("HW"), 0.0)
+    p0, r_, dm = A("PI", 0, 1), col(cR), A("DM", 0, 128)
+    w01, e0, e15 = col(2, name="LT"), col(0, name="EQJ"), col(15, name="EQJ")
     ts(A("PI", 1, 2), p0, 15, OP.bitwise_and)
     ts(A("PI", 2, 3), p0, 4, OP.arith_shift_right)
     for j in range(4):
-        ts(A("PI", 4 + j, 5 + j), p0, j, OP.arith_shift_right, 1, OP.bitwise_and)
+        ts(A("PI", 3 + j, 4 + j), p0, j, OP.arith_shift_right, 1, OP.bitwise_and)
+    copy(col(cR, 2), A("PI", 1, 3))
+    copy(col(cB, 4), A("PI", 3, 7))
+    for name, op in (("LT", OP.is_gt), ("EQJ", EQL), ("DJ", SUB)):
+        ts(A(name), A("J"), r_, op)
+    memset(A("HW"), 0.0)
+    lin(col(cG4), col(cG), float(E))
+    lin(col(cG1), col(cG), float(V))
+    lin(col(cSEL), e0, -1.0, 1.0)
+    lin(col(cS, 4), col(cB, 4), -1.0, 1.0)
+    lin(col(cW23), w01, -1.0, col(4, name="LT"))
+    lin(col(cSH), e15, -16.0, 1.0)
+    lin(col(cM), col(cSEL), -2048.0)
+    lin(col(cBIG), col(cSEL), BIG)
+    lin(col(cT), col(cS + 1), bias=col(cS + 2))
+    lin(col(cU), col(cS), col(cSEL))
+    lin(col(cBI + 1, 3), col(cB + 1, 3), BIG + 2048.0, col(cM))
+    lin(col(cN), col(cT), bias=col(cS + 3))
+    lin(col(cT), r_, -1.0, UP - E)
+    lin(col(cOFF), col(cN), col(cM))
+    lin(sm(NV), sm(VL), -1.0, col(cT))
+    lin(col(cDG), col(cU), -32768.0, col(cOFF))
+    lin(col(cN), col(cOFF), -1.0, -64.0)
+    lin(col(cBI), col(cB), BIG, col(cN))
+
     copy(A("LU1"), A("LV"))
-    copy(col(cR), A("PI", 1, 2))
-    copy(col(cG), A("PI", 2, 3))
-    copy(col(cB, 4), A("PI", 4, 8))
-    memset(A("IN", 252, 256), 0)
-    ts(col(cN0), col(cR), 0.5, OP.is_gt)
-    ts(col(cG4), col(cG), float(E), MUL)
-    ts(col(cG1), col(cG), float(V), MUL)
-    ts(col(cS, 4), col(cB, 4), -1.0, MUL, 1.0, ADD)
-    ts(col(c15), col(cR), -1.0, MUL, 15.0, ADD)
-    ts(col(cM), col(cN0), -2048.0, MUL)
-    tt(col(32, 2), col(cS, 2), col(cS + 2, 2), ADD)
-    ts(A("IN", 256, 508), A("IN", 256, 508), col(cG4), SUB)
-    ts(A("IN", 508, 592), A("IN", 508, 592), col(cG1), SUB)
-    ts(col(cBI, 4), col(cB, 4), 102048.0, MUL, col(cM), ADD)
-    ts(col(cBF), col(32), col(33), ADD, col(cM), MUL)
+    ts(A("IN", 252, 504), A("IN", 252, 504), col(cG4), SUB)
+    ts(A("IN", 504, 588), A("IN", 504, 588), col(cG1), SUB)
+    ts(A("M1"), A("DM"), col(15, name="DJ"), EQL)
     ts(A("ILO"), A("IN"), 63, OP.bitwise_and)
-    ts(A("IHI"), A("IN"), 6, OP.arith_shift_right)
-    ts(A("HDF"), A("IN", 0, 252), 64.0, ADD)
+    ts(A("IHI"), A("IN"), 4032, OP.bitwise_and)
+    ts(A("IDF"), dm, 0.0, EQL)
     copy(A("BLO"), A("ILO"))
     copy(A("BHI"), A("IHI"))
+    ts(A("HDF"), A("IN", 0, 252), 64.0, ADD)
     for k in KS:
         act(blk("SO", k, V), G(A("SPW", 0, E), blk("LU1", k)))
-    act(A("X0"), A("VROW"), ACT.Identity, bias=col(cBI), scale=col(cS))
-    act(A("XF"), A("VROW"), ACT.Identity, bias=col(cBF), scale=col(cN0))
-    act(A("V64"), A("VROW"), ACT.Identity, bias=64.0)
     order("y", [], [("HW", 0, E1)])
-    for r, name, a, b, lo, hi in ((0, "BLO", 0, 252, 0, E), (1, "BHI", 0, 252, 0, E), (2, "BLO", 256, 508, 0, E),
-                                  (3, "BHI", 256, 508, 0, E), (0, "BLO", 508, 592, E, E1), (1, "BHI", 508, 592, E, E1)):
-        dma("y", (T.HW[ROW[r], lo:hi], [("HWr%d" % r, lo, hi)]), A(name, a, b))
-    dma("y", A("YHW", 0, E, part=ROW[0]), A("HDF"))
-
-    ts(col(c1), col(cR), -1.0, MUL, 1.0, ADD)
-    ts(col(cN), col(cR), -1.0, MUL)
-    ts(col(cE0), col(cR), 0.0, EQL)
-    ts(col(cE15), col(cR), 15.0, EQL)
-    ts(col(cT), col(cR), 1.0, EQL, 64.0, MUL)
-    ts(col(34), col(cR), 2.0, EQL)
-    ts(col(35), col(cR), 3.0, EQL, 64.0, MUL)
-    copy(A("L1F"), A("LV"))
-    tt(col(cWP), col(cT), col(cE0), ADD)
-    tt(col(cWC), col(34), col(35), ADD)
-    tt(col(cWS), col(cN0), col(cE15), SUB)
-    ts(col(cNWP), col(cWP), -1.0, MUL)
-    for name, w in (("MK", 16384.0), ("MP", col(cWP)), ("MC", col(cWC)), ("MV", 8192.0), ("M0H", col(cE0)),
-                    ("M15H", col(cE15)), ("M1H", col(cN0)), ("M0F", col(cE0))):
-        ts(A(name), A("DM"), col(c15), EQL, w, MUL)
-    dm = A("DM", 0, 128)
-    for name, d, w in (("IDF", 0.0, 1.0), ("INJ", col(c1), col(cWP)), ("NINJ", col(c1), col(cNWP)),
-                       ("SH", 1.0, col(cWS)), ("IDN", 0.0, -8192.0), ("IDE", 0.0, -2.0 ** -20), ("IDS", 0.0, 2.0 ** -6)):
+    for r, name, a, b, lo, hi in ((0, "BLO", 0, 252, 0, E), (1, "BHI", 0, 252, 0, E), (2, "BLO", 252, 504, 0, E),
+                                  (3, "BHI", 252, 504, 0, E), (0, "BLO", 504, 588, E, E1), (1, "BHI", 504, 588, E, E1)):
+        dma("y", row(r, lo, hi), A(name, a, b))
+    ts(A("L1S"), A("LV"), UP, ADD)
+    memset(A("NEG", 0, 448), -1.0)
+    for name, w in (("MK", UP), ("MP", w01), ("MH", 1.0), ("M0H", e0)):
+        ts(A(name), A("M1"), w, MUL)
+    for name, w in (("IDN", -8192.0), ("IB", 1.0), ("IP", col(cSEL)), ("DG", col(cDG))):
+        ts(A(name), A("IDF"), w, MUL)
+    for name, d, w in (("INJ", col(1, name="DJ"), w01), ("I32", col(0, name="DJ"), w01), ("SH", col(cSH), col(cSEL))):
         ts(A(name), dm, d, EQL, w, MUL)
-    ts(A("TB1"), dm, col(cN), OP.is_ge, col(cWP), MUL)
-    ts(A("TB2"), dm, col(c15), OP.is_le)
-    ts(sm(VL), sm(VL), col(cR), ADD)
-    memset(A("NEG"), -1.0)
+    ts(A("TB2"), dm, col(15, name="DJ"), OP.is_le)
+    ts(A("TB1"), dm, col(0, name="DJ"), OP.is_ge, w01, MUL)
+    ts(A("TB3"), dm, 0.0, OP.is_gt, -32768.0, MUL)
     tt(A("BC"), A("TB1"), A("TB2"), MUL)
-    ts(sm(NV), sm(VL), -1.0, MUL, -float(E), ADD)
-    ts(sm(DB), sm(VL), E + 0.25, ADD)
-    ts(sm(DB2), sm(VL), E1 + 0.25, ADD)
-    copy(A("LN1"), A("LVN", 0, 252))
+    ts(A("TB1"), A("IDF"), 32768.0, MUL)
+    tt(A("TB3"), A("TB3"), A("TB2"), MUL)
+    copy(A("LN1"), A("LVN"))
+    tt(A("EM"), A("TB3"), A("TB1"), ADD)
+    lin(A("X0"), A("VROW"), col(cS), col(cBI))
 
-    def scatter_spins(a, b):
-        copy(G(A("YSW"), ul(TG1, a, b)), A("SPW", E + 16 * a, E + 16 * b))
+    def late_constants():
+        lin(A("MC"), A("M1"), col(cW23))
+        lin(A("NBC"), A("BC"), -1.0)
+        for name, w in (("IBM", -1.0), ("IDM", -1.0), ("IDE", -float(E))):
+            lin(A(name), A("IDF"), w)
+        for a, b in THIRDS[1:]:
+            act(part("NEG", a, b), part("NEG", 0, 28))
 
     def mirror(name, a, b):
-        dma("y", A("MD", 16 * a, 16 * b), A(name, 16 * a, 16 * b))
+        dma("y", part("MD", a, b), part(name, a, b))
 
-    def madd(out, win, j, more=True):
-        for a, b in THIRDS:
-            tt(A(out, 16 * a, 16 * b), G(A(win), ul(j, a, b)), A("MD", 16 * a, 16 * b), ADD)
-            if more:
+    HOP = ["P1", "PA", "PB", "PA", "PB", "PA"]
+    MW = ["MS", "MA", "MB", "MA", "MB"]
+    WW = ["WB", "WA", "WB", "WA", "WB", "TT"]
+    PASS = {"DG": ("R", "NEG", True, False), "BC": ("R", "P1", False, True),
+            "NBC": ("Q", "HW", True, False), "I32": ("Q", "PA", False, False), "IP": ("Q", "TT", False, True),
+            "INJ": ("R", "PB", True, False), "SH": ("R", "TT", False, False), "EM": ("R", "EQ", False, True)}
+
+    def step(name, last):
+        wid = E1 if last else E
+        lf, up = ("LMX", -E - 15 * UP) if last else ("L1S", UP)
+        m32 = "M32B" if last else "M32A"
+        low = wid + 16 * UP
+        j = int(name[1]) if name[1:2].isdigit() else None
+        i = int(name[-1]) if name[-1].isdigit() and (len(name) > 2 or name[0] in "gqky") else None
+        a, b = THIRDS[i] if i is not None and i < 3 else (0, C)
+        if name == "P1":
+            act(A("P1"), G(HWW(0, wid), ul(ENT)))
+        elif name[:2] in ("Pv", "Ps"):
+            a, b = (0, OPT["p1"]) if name == "Pv" else (OPT["p1"], C)
+            (act if name[1] == "s" else copy)(part("P1", a, b), G(HWW(0, wid), ul(ENT, a, b)))
+        elif name[:2] in ("Mv", "Ms"):
+            (act if name[1] == "s" else copy)(part("MS", a, b), G(A("SPW", 0, wid), ul(ENT, a, b)))
+            if last:
+                mirror("MS", a, b)
+        elif name == "neg":
+            ts(A("SPW", E, E1), A("MS"), -1.0, MUL)
+        elif name == "snd":
+            order("g", [("MB", 0, V), ("MD", 0, V)], [])
+            send("SNW", A("SPW", E, E1), E, E1, "arrM")
+        elif name == "app":
+            if not last:
+                for r in (2, 3):
+                    dma("y", row(r, E, E1), A("P1", part=ROW[r]))
+            order("g", A("UL", PL * C, (PL + 5) * C)[1], [])
+            dma("g", A("EW", wid, wid + V, part=ROW[0]), A("P1", part=ROW[2]))
+            dma("g", A("EW", wid, wid + V, part=ROW[0]), A("P1", part=ROW[3]), accum_op=ADD)
+        elif name == "ENS":
+            ts(sm(ENS), si(4), up, ADD)
+        elif name == "D":
+            mm(ps("Q0", 0, 3), [(A("IDF"), A(lf))], stop=False)
+            for k in range(3):
+                mm(ps("Q0", k, k + 1), [(A("IDM"), sm(ENS))], start=False, stop=k == 2)
+        elif name == "PEN":
+            act(A("PEN"), ps("Q0", 0, 3), ACT.Abs, scale=32768.0)
+        elif name == "pen":
+            mm(ps("Q0", 0, 3), [(A("IBM"), A("PEN"))], stop=False)
+        elif name == "MC":
+            conv("Q1", "MC", "P1")
+        elif name == "NC":
+            lin(sm(NC_), *((ps("Q1"), -1.0, UP - low) if last else (sm(ENS), -1.0, 2 * UP - low)))
+        elif name == "NV":
+            lin(sm(NV), sm(NV), bias=-float(V) if last else -low)
+        elif name == "HD":
+            act(A("HDF"), A("HDF"), ACT.Silu)
+            dma("y", A("YHW", 0, E, part=ROW[0]), A("HDF"))
+        elif name == "LF":
+            lin(A("LFL"), A(lf), bias=UP - up - low)
+        elif name.split("_")[0] in PASS:
+            mat = name.split("_")[0]
+            bank, src_, start, stop = PASS[mat]
+            for k, (a, b) in enumerate(THIRDS):
+                if "_" not in name or k == i:
+                    x = HWW(E + 16 * a, E + 16 * b) if src_ == "HW" else \
+                        part(src_, 0, 28) if src_ == "NEG" else part(src_, a, b)
+                    mm(A("%s%d" % (bank, k), 0, 448), [(A(mat), x)], start=start, stop=stop)
+        elif name[0] == "c" and j is not None:
+            conv("L%d" % (j % 2), "MP", HOP[j])
+        elif name[0] == "l" and j is not None:
+            copy(ul(PL + j), ps("L%d" % (j % 2)))
+        elif name[0] == "h" and j is not None:
+            act(part(HOP[j + 1], a, b), G(A(HOP[j]), ul(PL + j, a, b)))
+        elif name[0] == "H":
+            copy(part(HOP[j + 1], a, b), G(A(HOP[j]), ul(PL + j, a, b)))
+        elif name[0] == "m" and j is not None:
+            out, neg = (m32 if j == 4 else MW[j + 1]), j == 0 and not last
+            tt(part(out, a, b), G(A(MW[j]), ul(PL + j, a, b)), part("SPW", a, b, E) if neg else part("MD", a, b),
+               SUB if neg else ADD)
+            if j < 3 or j == 3 and "m4%d" % i in ORDER[last]:
                 mirror(out, a, b)
+        elif name[0] == "w" and j == 0:
+            tt(part("WA", a, b), A("R%d" % i, 0, 448), part("X0", a, b), MIN)
+        elif name[0] == "w":
+            tt(part(WW[j + 1], a, b), G(A(WW[j]), ul(PL + j, a, b)), part("X", a, b), MIN)
+        elif name[0] == "x":
+            lin(part("X", a, b), part(WW[j], a, b), *((e0, col(cBIG)) if j == 4 else (col(cS + j), col(cBI + j))))
+        elif name[0] == "g":
+            act(part("MD", a, b), G(A("MB"), ul(PL + 4, a, b)))
+        elif name[0] == "q":
+            mm(A("L0", 0, 448), [(A("IB"), part(x, a, b)) for x in ("MB", "MD")])
+        elif name[0] == "k":
+            act(part(m32, a, b), A("L0", 0, 448))
+        elif name == "low":
+            conv("L1", "M0H", "TT")
+        elif name[:2] == "eq":
+            ts(part("EQ", a, b), A("Q%d" % i, 0, 448), 0.0, EQL)
+        elif name[:2] == "es":
+            act(A("AB"), A("Q%d" % i, 0, 448), ACT.Abs)
+            act(part("EQ", a, b), A("AB"), ACT.Relu, scale=-1.0, bias=1.0)
+        elif name == "min":
+            copy(ul(LOWU), ps("L1"))
+        elif name[:3] == "pov" or name == "pos0":
+            ts(part("POS", a, b), G(A(m32), ul(LOWU, a, b)), 0.5, OP.is_gt, -0.5, ADD)
+        elif name[:3] in ("pos", "POS"):
+            act(part("POS", a, b), G(A(m32), ul(LOWU, a, b)), ACT.Sign, bias=-0.5)
+        elif name[0] == "y":
+            ts(part("PD", a, b), A("R%d" % i, 0, 448), -32768.0, ADD, -UP, MAX)
+        elif name == "cy":
+            conv("L0", "MH", "PD")
+        elif name == "cv":
+            conv("L1", "MK", "POS")
+        elif name == "VV":
+            lin(sm(EE), ps("L1"), bias=1.5 * UP - low)
+        elif name[:2] == "sc":
+            a, b = OPT["sc"][i:i + 2]
+            copy(G(A("YSW"), ul(TG1, a, b)), part("SPW", a, b, E))
+        else:
+            assert name[:2] == "hs", name
+            a, b = OPT["hs"][i:i + 2]
+            act(G(A("YHW"), ul(TG1, a, b)), part("VROW", a, b), ACT.Silu)
 
     for rnd in range(2):
         last = rnd == 1
         wid = E1 if last else E
-        ln, lf = ("LN2", "L2F") if last else ("LN1", "L1F")
+        ln, lf = ("LN2", "LMX") if last else ("LN1", "L1S")
         m32 = "M32B" if last else "M32A"
-        KB = {1: "L0", 2: "L1", 0: "L2"}
+        KB = {1: "L0", 2: "L1", 0: "Q2"}
 
         for k in KS:
-            mm(ps(KB[k]), [(A("IDF"), blk(lf, k))] + ([(A("IDN"), A("NEG", 0, C))] if k != 2 else []), stop=False)
+            mm(ps(KB[k]), [(A(x), A("NEG", 0, C)) for x in ["IDN"] * (k != 2) + ["IDE"] * last] +
+               [(A("IDF"), blk(lf, k))], stop=False)
+        P9 = [(k, a, b) for k in KS for a, b in THIRDS]
+        nh = 0 if last else OPT["help"]
+        HB = dict(zip(P9[9 - nh:], ["R0", "R1", "R2", "Q0", "Q1"]))
+        for (k, a, b), bank in HB.items():
+            mm(A(bank, 0, 448), [(A("IB"), part("SO", a, b, k * V))])
+            act(part("YLW", a, b, k * V), G(A("SNW", 0, wid), A(ln, k * C + a, k * C + b)))
         for k in KS:
-            tt(blk("PR", k, V), G(A("SNW", 0, wid), blk(ln, k)), blk("SO", k, V), MUL)
+            own = [x for x in P9 if x[0] == k and x not in HB]
+            if own:
+                a, b = own[0][1], own[-1][2]
+                tt(part("PR", a, b, k * V), G(A("SNW", 0, wid), A(ln, k * C + a, k * C + b)),
+                   part("SO", a, b, k * V), MUL)
+            for x in HB:
+                if x[0] == k:
+                    tt(part("PR", x[1], x[2], k * V), A(HB[x], 0, 448), part("YLW", x[1], x[2], k * V), MUL)
             conv(KB[k], "MK", "PR", k * V, start=False)
             if k == 2:
                 copy(si(0), ps("L0"))
         if not last:
+            late_constants()
             order("y", [("SNW", 0, E)], [])
             dma("y", A("YSW", 0, E), H("sp", T.sp[:]))
-        tt(si(1), ps("L1"), si(0), OP.max)
+        tt(si(1), ps("L1"), si(0), MAX)
         ts(si(2), si(1), -8193, OP.bitwise_and)
-        tt(si(3), ps("L2"), si(2), OP.max)
+        if last and OPT["sc"][3] < C:
+            step("sc3", last)
+        tt(si(3), ps("Q2"), si(2), MAX)
         ts(si(4), si(3), 8191, OP.bitwise_and)
         copy(ul(ENT), si(4))
 
-        act(A("P1"), G(HWW(0, wid), ul(ENT)))
-        for a, b in THIRDS:
-            (act if b == C or last and a else copy)(A("MS", 16 * a, 16 * b), G(A("SPW", 0, wid), ul(ENT, a, b)))
-            mirror("MS", a, b)
-        if last:
-            scatter_spins(C // 2, C)
-        conv("L3", "MP", "P1")
-        for b, lo, hi in RB:
-            mm(A(b, 0, hi - lo), [(A("BC"), A("P1", lo, hi))])
-        for k in range(3):
-            tt(blk("OH", k), blk(lf, k), si(4), EQL)
-        copy(ul(PL), ps("L3"))
-        act(A("PA"), G(A("P1"), ul(PL)))
-        for b, lo, hi in RB:
-            tt(A("WA", lo, hi), A(b, 0, hi - lo), A("X0", lo, hi), OP.min)
-        conv("L4", "MP", "PA")
-        if last:
-            conv("L0", "MC", "P1")
-        madd("MA", "MS", PL)
-        if not last:
-            ts(sm(NC_), si(4), -1.0, MUL)
-        for b, lo, hi in RB:
-            mm(A(b, 0, hi - lo), [(A("NINJ"), (T.HW[:, E + lo:E + hi], HWW(E, E1)[1]))], stop=False)
+        for name in ORDER[rnd].split():
+            step(name, last)
 
-        pw, ww, mw, lb = ["PA", "PB"], ["WA", "WB"], ["MA", "MB"], ["L4", "L3"]
-        for j in (1, 2, 3):
-            a, b = (j - 1) % 2, j % 2
-            act(A("X"), A(ww[a]), ACT.Identity, bias=col(cBI + j), scale=col(cS + j))
-            copy(ul(PL + j), ps(lb[a]))
-            act(A(pw[b]), G(A(pw[a]), ul(PL + j)))
-            conv(lb[b], "MP", pw[b])
-            tt(A(ww[b]), G(A(ww[a]), ul(PL + j)), A("X"), OP.min)
-            madd(mw[b], mw[a], PL + j)
-            if j == 3 and last:
-                act(sm(NC_), ps("L0"), scale=-1.0)
-        for b, lo, hi in RB:
-            mm(A(b, 0, hi - lo), [(A("INJ"), A("PB", lo, hi))], start=False, stop=False)
-        conv("L1", "M0F", "WB")
-
-        copy(ul(PL + 4), ps("L3"))
-        act(A("PA"), G(A("PB"), ul(PL + 4)))
-        if last:
-            act(A("EW", E1, E2), G(A("EW", 0, E1), ul(ENT)))
-        else:
-            act(A("SPW", E, E1), A("MS"), scale=-1.0)
-            send("SNW", A("SPW", E, E1), E, E1, "arrM")
-            for r in (2, 3):
-                dma("y", (T.HW[ROW[r], E:E1], [("HWr%d" % r, E, E1)]), A("P1", part=ROW[r]))
-        act(sm(LOWN), ps("L1"))
-        tt(A("TT"), G(A("WB"), ul(PL + 4)), A("XF"), SUB)
-        conv("L0", "M0H", "TT")
-        for b, lo, hi in RB:
-            mm(A(b, 0, hi - lo), [(A("SH"), A("TT", lo, hi))], start=False)
-        conv("L2", "M15H", "TT")
-        conv("L3", "MP", "PA")
-        madd(m32, "MB", PL + 4, False)
-        tt(sm(LOW), ps("L0"), sm(LOWN), OP.min)
-        copy(ul(LOWU), sm(LOW))
-        act(A("POS"), G(A(m32), ul(LOWU)), ACT.Sign, bias=-0.5)
-        if not last:
-            act(A("EW", E, E1), G(A("EW", 0, E), ul(ENT)))
-        ts(A("EQ"), A("TT"), 0.0, EQL)
-        mm(ps("L4"), [(A("IDE"), A("NEG", 0, C))], stop=False)
-        mm(ps("L0"), [(A("IDS"), A("NEG", 0, C))], stop=False)
-        conv("L4", "M1H", "EQ", start=False)
-        for b, lo, hi in RB:
-            tt(A("PD", lo, hi), A(b, 0, hi - lo), A("EQ", lo, hi), MUL)
-        mm(ps("L1"), [(A("IDN"), A("NEG", 0, C))], stop=False)
-        conv("L0", "M1H", "PD", start=False)
-        conv("L1", "MV", "POS", start=False)
         if last:
             dma("g", H("yw", T.yw[:]), A(m32), accum_op=ADD)
-        tt(sm(EQ32), ps("L3"), sm(VL), EQL)
-        tt(sm(CNT), ps("L4"), sm(EQ32), ADD)
-        tt(sm(U), ps("L2"), sm(EQ32), MUL)
-        run("v", sm(REC), [sm(CNT)], lambda: g.vector.reciprocal(sm(REC)[0], sm(CNT)[0]))
-        tt(sm(SU), ps("L0"), sm(U), ADD)
+        low = wid + 16 * UP
+        tt(sm(FF), ps("L0"), sm(EE), MIN)
+        for k in range(3):
+            mm(ps("Q0", k, k + 1), [(A("IDF"), sm(FF))], start=False, stop=k == 2)
         tg = TG2 if last else TG1
         lu = "LU3" if last else "LU2"
-
-        def targets(step):
-            if step == 1:
-                tt(sm(ZZ), sm(FF), sm(NC_), OP.min)
-            elif step == 2:
-                tt(sm(NT), sm(ZZ), sm(NV), OP.max)
-            else:
-                ts(ul(tg), sm(NT), -1.0, MUL)
-
-        tt(sm(QQ), sm(SU), sm(REC), MUL)
-        tt(sm(EE), sm(QQ), sm(DB2 if last else DB), ADD)
-        tt(sm(FF), ps("L1"), sm(EE), OP.min)
+        tt(sm(ZZ), sm(FF), sm(NC_), MIN)
+        tt(sm(NT), sm(ZZ), sm(NV), MAX)
         if last:
-            for step in (1, 2, 3):
-                targets(step)
-            act(G(A("YHW"), ul(tg)), A("V64"), ACT.Silu)
+            ts(ul(tg), sm(NT), -1.0, MUL, UP - low, ADD)
+            act(G(A("YHW"), ul(tg)), A("VROW"), ACT.Silu)
             dma("s", A("HDF"), A("YHW", 0, E, part=ROW[0]))
-        for k in range(3):
-            tt(blk("CAND", k), blk("OH", k), sm(FF), MUL)
-        tt(A("LMX"), A("CAND"), A(lf), OP.max)
-        copy(A(lu), A("LMX"))
+            if not OPT["lu_first"]:
+                tt(G(A("YSW"), ul(tg)), A("MS"), A("NEG"), MUL)
+        tt(A("LMX"), ps("Q0", 0, 3), A("LFL"), MAX)
+        ts(A(lu), A("LMX"), low - UP, ADD)
         if not last:
             send("LN2", A("LU2"), 0, 252, "arrN")
             for k in KS:
                 act(blk("SO", k, V), G(A("SPW"), blk("LU2", k)))
-            targets(1)
-            copy(A("L2F"), A("LU2"))
-            targets(2)
-            targets(3)
+            ts(ul(tg), sm(NT), -1.0, MUL, UP - low, ADD)
             dma("g", H("yw", T.yw[:]), A(m32))
-            scatter_spins(0, C // 2)
-            act(G(A("YHW"), ul(tg)), A("V64"), ACT.Silu)
+            for name in AFTER.split():
+                step(name, last)
         else:
-            tt(G(A("YSW"), ul(tg)), A("MS"), A("NEG"), MUL)
+            if OPT["lu_first"]:
+                tt(G(A("YSW"), ul(tg)), A("MS"), A("NEG"), MUL)
             dma("y", H("ys", T.ys[:]), A("YSW", 0, E))
-            for f, q, a, b in ((act, "s", 0, 168), (copy, "y", 168, 252)):
-                f(A("YLW", 16 * a, 16 * b), G(A("EW"), A("LU3", a, b)))
-                dma(q, H("yl%d" % a, T.yl[:, 16 * a:16 * b]), A("YLW", 16 * a, 16 * b, part=ROW[0]))
-            copy(A("ILO", 0, 252), A("HDF"))
-            ts(A("HR1"), A("ILO", 0, 252), -64.0, ADD)
-            dma("y", H("yh", T.yh[:]), A("HR1"))
+            for f, q, a, b in ((act, "s", 0, OPT["yl"]), (copy, "y", OPT["yl"], OPT["yh"]), (copy, "y", OPT["yh"], 252)):
+                if a == OPT["yh"]:
+                    ts(A("HR1"), A("HDF"), 12582912.0, ADD, -12582976.0, ADD)
+                    dma("y", H("yh", T.yh[:]), A("HR1"))
+                if a < b:
+                    f(A("YLW", 16 * a, 16 * b), G(A("EW"), A("LU3", a, b)))
+                    dma(q, H("yl%d" % a, T.yl[:, 16 * a:16 * b]), A("YLW", 16 * a, 16 * b, part=ROW[0]))
 
     total["sent"] = sent[0]
     for s in sorted(total):

from concourse.bass import DstId, RemoteDMATransfer
from concourse.mybir import AluOpType, ActivationFunctionType

V, E, C = 1344, 4032, 84
E1, E2 = E + V, E + 2 * V
BF, F32, F16, I32, U16 = "bfloat16", "float32", "float16", "int32", "uint16"
CUT = [0, 1728, 3456, E]
NCH = len(CUT) - 1
UP = 16384.0
OPT = dict(yl=140, yh=224, sc=(0, 48, 70, 76, 84), hs=(0, 72, 84), p1=42, lu_first=True, help=5)

WALK = ("DG P1 Mv0 Mv1 Mv2:0 Ms2:1 NV c0 BC ENS MC:1 neg:0 sc1:1 l0 h0 sc2:1 w00 w01 w02 x1 c1 m00 m01 l1 h1 m02 "
        "w1 D c2 x2 m10 m11 l2 app h2 NC:1 m12 w2 c3 PEN x3 NBC m20 m21 l3 h3 LF:1 m22 c4 "
        "w3 x4 m30 m31 l4 h4 m32 g2 snd:0 INJ "
        "w40 SH_0 w41 SH_1 w42 I32_0 IP_0 q2 k2 low I32_1 IP_1 I32_2 IP_2 SH_2 m40 m41 min POS hs1:1 LF:0 NC:0 "
        "eq0 eq1 EM_0 EM_1 eq2 EM_2 y0 y1 y2 cv VV HD:0 pen cy")
ORDER = [" ".join(x.split(":")[0] for x in WALK.split() if x.split(":")[-1] != str(1 - r)) for r in range(2)]
AFTER = "sc0 hs0"

SCRATCH = {}
for _d, _w, _names in [
    (BF, E1, "SPW SNW YSW HW"), (F32, E1, "YHW"), (F32, E2, "EW"), (BF, E, "SO PR"), (F32, E, "YLW"),
    (F32, V, "VROW X0 X WA WB"), (BF, V, "MS MA MB MD M32A M32B P1 PA PB POS NEG EQ"), (F16, V, "TT PD"),
    (I32, 252, "LV LVN"), (I32, 588, "IN ILO IHI"), (BF, 588, "BLO BHI"),
    (U16, 252, "LU1 LN1 LU2 LN2 LU3"), (U16, C * 9, "UL"), (F32, 252, "HDF HR1 L1S L2S LFL LMX"), (BF, 252, "PEN"),
    (F32, C * 12, "SM"), (I32, C * 5, "SI"), (F32, 144, "DM M1"), (I32, 8, "PI"),
    (F32, 32, "COL"), (F32, 16, "J LT EQJ DJ"), (F32, 128, "TB1 TB2 TB3 IDF IDM"), (BF, 144, "MP MC MK"),
    (F16, 144, "M0H MH"), (F16, 128, "SH IP"), (BF, 128, "EM BC NBC INJ I32 DG IB IBM IDN IDE"), (BF, 448, "AB"),
]:
    for _n in _names.split():
        SCRATCH[_n] = ("sbuf", [128, _w], _d)
for _n in ("R0", "R1", "R2", "Q0", "Q1", "Q2", "L0", "L1"):
    SCRATCH[_n] = ("psum", [128, 512], F32)

SEMAPHORES = ["ev", "es", "et", "eg", "sent", "arrL", "arrS", "arrM", "arrN", "hL"] + \
    ["h%d" % i for i in range(NCH - 1)] + ["d%d" % i for i in range(60)]

OP = AluOpType
ACT = ActivationFunctionType


def helper_of(src, dst, T, topo):
    if topo.chip(src) == topo.chip(dst):
        return None
    for h in topo.cores_of(src):
        if T.rank_of(h) is None and topo.die(h) != topo.die(src) and topo.may_write(h, dst):
            return h
    return None


def bits(m):
    return bin(m).count("1")


def pieces():
    return [("LV", "LVN", 0, 126, 252, "hL", "arrL")] + \
        [("SPW", "SNW", CUT[i], (CUT[i] + CUT[i + 1]) // 2, CUT[i + 1], "h%d" % i, "arrS") for i in range(NCH)]


def helper_program(g, core, src, dst, T, topo):
    rid, pid, _ = topo.addr(dst)
    m = topo.mask(core, dst)
    inc = bits(topo.mask(src, core) & ~topo.mask(src, dst))
    n = 0
    for _, land, a, b, c, hs, arr in pieces()[:-1]:
        g.wait_ge(T.sem[hs], inc)
        g.remote_dma(T[land][:, b:c], T[land][:, b:c], T.sem[arr], T.sem.sent, pid, rid, m)
        n += bits(m)
    g.wait_ge(T.sem.sent, n)


def rank_program(g, core, T, topo):
    n_rank = len(T.cores)
    rank = T.rank_of(core)
    if rank is None:
        for r in range(n_rank):
            src, dst = T.cores[r], T.cores[(r - 1) % n_rank]
            if helper_of(src, dst, T, topo) == core:
                helper_program(g, core, src, dst, T, topo)
        return
    dst = T.cores[(rank - 1) % n_rank]
    src = T.cores[(rank + 1) % n_rank]
    hout = helper_of(core, dst, T, topo)
    hin = helper_of(src, core, T, topo)
    in_direct = bits(topo.mask(src, core))
    in_piece = in_direct + (bits(topo.mask(hin, core)) if hin is not None else 0)

    Q = {"v": g.vector, "s": g.scalar, "t": g.tensor, "g": g, "y": g.sync}
    total = {}
    known = {q: {} for q in Q}
    hist = {}
    ndma = [0]

    def wait(q, tok):
        sem, val, clock = tok
        if known[q].get(sem, 0) >= val:
            return
        Q[q].wait_ge(T.sem[sem], val)
        known[q][sem] = val
        for s, x in clock.items():
            if known[q].get(s, 0) < x:
                known[q][s] = x

    def order(q, reads, writes, cont=False):
        toks = []
        for regs, wr in ((reads, False), (writes, True)):
            for name, lo, hi in regs:
                psum = name in SCRATCH and SCRATCH[name][0] == "psum"
                for (l2, h2, w2, q2, tok) in hist.get(name, []):
                    if psum:
                        if q2 == q and (q == "t" and cont or not (wr or w2)):
                            continue
                        toks.append(tok)
                    elif l2 < hi and lo < h2 and (wr or w2):
                        toks.append(tok)
        toks.sort(key=lambda t: -t[1])
        for tok in toks:
            wait(q, tok)

    def note(q, reads, writes, tok):
        for name, lo, hi in writes:
            hist[name] = [x for x in hist.get(name, []) if not (lo <= x[0] and x[1] <= hi)] + [(lo, hi, True, q, tok)]
        for name, lo, hi in reads:
            hist.setdefault(name, []).append((lo, hi, False, q, tok))

    def run(q, out, ins, call, cont=False):
        w, r = out[1][:1], out[1][1:]
        for x in ins:
            r = r + x[1]
        order(q, r, w, cont)
        sem = "e" + q
        total[sem] = total.get(sem, 0) + 1
        call().then_inc(T.sem[sem], 1)
        note(q, r, w, (sem, total[sem], dict(known[q])))

    def A(name, lo=0, hi=None, step=None, part=None):
        hi = SCRATCH[name][1][1] if hi is None else hi
        cols = slice(lo, hi) if step is None else slice(lo, hi, step)
        return (T[name][part if part is not None else slice(None), cols], [(name, lo, hi)])

    def G(win, off):
        return (win[0].indirect(off[0]), win[1] + off[1])

    def sc(x):
        return x if isinstance(x, tuple) else (x, [])

    def copy(out, a):
        run("v", out, [a], lambda: g.vector.tensor_copy(out[0], a[0]))

    def tt(out, a, b, op):
        run("v", out, [a, b], lambda: g.vector.tensor_tensor(out[0], a[0], b[0], op))

    def ts(out, a, s1, op0, s2=None, op1=None):
        s1, s2 = sc(s1), sc(s2)
        ops = [op0] if op1 is None else [op0, op1]
        run("v", out, [a, s1, s2], lambda: g.vector.tensor_scalar(out[0], a[0], s1[0], s2[0], *ops))

    def memset(out, c):
        run("v", out, [], lambda: g.vector.memset(out[0], c))

    def act(out, a, func=ACT.Copy, **kw):
        kw = {k: sc(x) for k, x in kw.items()}
        run("s", out, [a] + list(kw.values()),
            lambda: g.scalar.activation(out[0], a[0], func, **{k: x[0] for k, x in kw.items()}))

    def lin(out, a, scale=1.0, bias=0.0):
        act(out, a, ACT.Identity, scale=scale, bias=bias)

    def iota(out, pattern, cm, flt=False, base=0):
        kw = {"allow_small_or_imprecise_dtypes": True} if flt else {}
        run("g", out, [], lambda: g.iota(out[0], pattern, base, cm, **kw))

    def mm(out, pairs, start=True, stop=True):
        def call():
            ins = None
            for i, (l, x) in enumerate(pairs):
                ins = g.tensor.matmul(out[0], l[0], x[0], start and i == 0, stop and i == len(pairs) - 1)
            return ins
        run("t", out, [x for p in pairs for x in p], call, cont=not start)

    def conv(bank, master, name, lo=0, start=True, stop=True, at=0):
        mm(A(bank, at, at + C), [(A(master, 15 - i, 143 - i), A(name, lo + i, lo + V, 16)) for i in range(16)],
           start=start, stop=stop)

    def dma(q, out, in_, **kw):
        order(q, in_[1], out[1])
        sem = "d%d" % ndma[0]
        ndma[0] += 1
        Q[q].dma_start(out[0], in_[0], **kw).then_inc(T.sem[sem], 16)
        total[sem] = 16
        note(q, in_[1], out[1], (sem, 16, dict(known[q])))

    def H(name, ap):
        return (ap, [(name, 0, 1)])

    def arrival(name, lo, hi, sem, val):
        total[sem] = val
        note("r", [], [(name, lo, hi)], (sem, val, {}))

    sent = [0]
    rid, pid, _ = topo.addr(dst)
    mdir = topo.mask(core, dst)

    def send(land, src_ap, lo, hi, arr):
        order("g", src_ap[1], [])
        g.remote_dma(T[land][:, lo:hi], src_ap[0], T.sem[arr], T.sem.sent, pid, rid, mdir)
        sent[0] += bits(mdir)

    def send_piece(p):
        name, land, a, b, c, hs, arr = p
        if hout is None or c == E:
            send(land, A(name, a, c), a, c, arr)
            return
        order("g", A(name, a, c)[1], [])
        hrid, hpid, _ = topo.addr(hout)
        mh = topo.mask(core, hout) & ~mdir
        g.remote_dma_fused([
            RemoteDMATransfer(dst_ids=[DstId(rid=rid, pnc=pid)], dma_engine_mask=mdir, remote_sem=T.sem[arr],
                              src=T[name][:, a:b], dst=T[land][:, a:b]),
            RemoteDMATransfer(dst_ids=[DstId(rid=hrid, pnc=hpid)], dma_engine_mask=mh, remote_sem=T.sem[hs],
                              src=T[name][:, b:c], dst=T[land][:, b:c])], local_sem=T.sem.sent)
        sent[0] += bits(mdir) + bits(mh)

    arrival("LVN", 0, 252, "arrL", in_piece)
    arrival("SNW", 0, E, "arrS", in_piece * (NCH - 1) + in_direct)
    arrival("SNW", E, E1, "arrM", in_direct)
    arrival("LN2", 0, 252, "arrN", in_direct)

    def blk(name, k, w=C, a=0, b=None):
        return A(name, k * w + a, k * w + (w if b is None else b))

    def sm(i, n=1):
        return A("SM", i * C, (i + n) * C)

    def si(i, n=1):
        return A("SI", i * C, (i + n) * C)

    def ul(i, a=0, b=C):
        return blk("UL", i, C, a, b)

    def col(i, n=1, name="COL"):
        return A(name, i, i + n)

    def ps(name, a=0, b=1):
        return A(name, a * C, b * C)

    def part(name, a, b, lo=0):
        return A(name, lo + 16 * a, lo + 16 * b)

    def HWW(lo, hi):
        return (T.HW[:, lo:hi], [("HW", lo, hi)] + [("HWr%d" % r, lo, hi) for r in range(4)])

    def row(r, lo, hi):
        return (T.HW[ROW[r], lo:hi], [("HWr%d" % r, lo, hi)])

    ROW = [slice(r, 128, 16) for r in range(4)]
    THIRDS = [(0, 28), (28, 56), (56, C)]
    (VL, NV, NC_, ENS, NT, EE, FF, ZZ, LOWN, LOW, EQ32, U) = range(12)
    ENT, LOWU, TG1, TG2, PL = 0, 1, 2, 3, 4
    (cR, cG, cG4, cG1, cSEL, cW23, cOFF, cBIG, cDG, cSH, cM, cT, cU, cN) = range(14)
    BIG = 100000.0
    cB, cS, cBI = 16, 20, 24
    KS = (1, 2, 0)
    EQL, MUL, ADD, SUB, MIN, MAX = OP.is_equal, OP.mult, OP.add, OP.subtract, OP.min, OP.max

    P = pieces()
    dma("y", A("LV"), H("lv", T.lv[:]))
    dma("s", A("IN", 0, 252), H("hd", T.hd[:]))
    for p in P[1:]:
        dma("y", A("SPW", p[2], p[4]), H("sp", T.sp[:, p[2]:p[4]]))
    iota(A("PI", 0, 1), [[1, 1]], 1)
    iota(A("J"), [[1, 16]], 0, True)
    iota(A("DM"), [[1, 144]], -1, True)
    iota(A("IN", 252, 504), [[1, 252]], 252)
    iota(A("IN", 504, 588), [[1, C]], C)
    iota(sm(VL), [[16, C]], 0, True)
    for p in P:
        send_piece(p)
    iota(A("VROW"), [[1, V]], 0, True, 64)
    iota(A("EW"), [[1, E2]], 0, True)

    p0, r_, dm = A("PI", 0, 1), col(cR), A("DM", 0, 128)
    w01, e0, e15 = col(2, name="LT"), col(0, name="EQJ"), col(15, name="EQJ")
    ts(A("PI", 1, 2), p0, 15, OP.bitwise_and)
    ts(A("PI", 2, 3), p0, 4, OP.arith_shift_right)
    for j in range(4):
        ts(A("PI", 3 + j, 4 + j), p0, j, OP.arith_shift_right, 1, OP.bitwise_and)
    copy(col(cR, 2), A("PI", 1, 3))
    copy(col(cB, 4), A("PI", 3, 7))
    for name, op in (("LT", OP.is_gt), ("EQJ", EQL), ("DJ", SUB)):
        ts(A(name), A("J"), r_, op)
    memset(A("HW"), 0.0)
    lin(col(cG4), col(cG), float(E))
    lin(col(cG1), col(cG), float(V))
    lin(col(cSEL), e0, -1.0, 1.0)
    lin(col(cS, 4), col(cB, 4), -1.0, 1.0)
    lin(col(cW23), w01, -1.0, col(4, name="LT"))
    lin(col(cSH), e15, -16.0, 1.0)
    lin(col(cM), col(cSEL), -2048.0)
    lin(col(cBIG), col(cSEL), BIG)
    lin(col(cT), col(cS + 1), bias=col(cS + 2))
    lin(col(cU), col(cS), col(cSEL))
    lin(col(cBI + 1, 3), col(cB + 1, 3), BIG + 2048.0, col(cM))
    lin(col(cN), col(cT), bias=col(cS + 3))
    lin(col(cT), r_, -1.0, UP - E)
    lin(col(cOFF), col(cN), col(cM))
    lin(sm(NV), sm(VL), -1.0, col(cT))
    lin(col(cDG), col(cU), -32768.0, col(cOFF))
    lin(col(cN), col(cOFF), -1.0, -64.0)
    lin(col(cBI), col(cB), BIG, col(cN))

    copy(A("LU1"), A("LV"))
    ts(A("IN", 252, 504), A("IN", 252, 504), col(cG4), SUB)
    ts(A("IN", 504, 588), A("IN", 504, 588), col(cG1), SUB)
    ts(A("M1"), A("DM"), col(15, name="DJ"), EQL)
    ts(A("ILO"), A("IN"), 63, OP.bitwise_and)
    ts(A("IHI"), A("IN"), 4032, OP.bitwise_and)
    ts(A("IDF"), dm, 0.0, EQL)
    copy(A("BLO"), A("ILO"))
    copy(A("BHI"), A("IHI"))
    ts(A("HDF"), A("IN", 0, 252), 64.0, ADD)
    for k in KS:
        act(blk("SO", k, V), G(A("SPW", 0, E), blk("LU1", k)))
    order("y", [], [("HW", 0, E1)])
    for r, name, a, b, lo, hi in ((0, "BLO", 0, 252, 0, E), (1, "BHI", 0, 252, 0, E), (2, "BLO", 252, 504, 0, E),
                                  (3, "BHI", 252, 504, 0, E), (0, "BLO", 504, 588, E, E1), (1, "BHI", 504, 588, E, E1)):
        dma("y", row(r, lo, hi), A(name, a, b))
    ts(A("L1S"), A("LV"), UP, ADD)
    memset(A("NEG", 0, 448), -1.0)
    for name, w in (("MK", UP), ("MP", w01), ("MH", 1.0), ("M0H", e0)):
        ts(A(name), A("M1"), w, MUL)
    for name, w in (("IDN", -8192.0), ("IB", 1.0), ("IP", col(cSEL)), ("DG", col(cDG))):
        ts(A(name), A("IDF"), w, MUL)
    for name, d, w in (("INJ", col(1, name="DJ"), w01), ("I32", col(0, name="DJ"), w01), ("SH", col(cSH), col(cSEL))):
        ts(A(name), dm, d, EQL, w, MUL)
    ts(A("TB2"), dm, col(15, name="DJ"), OP.is_le)
    ts(A("TB1"), dm, col(0, name="DJ"), OP.is_ge, w01, MUL)
    ts(A("TB3"), dm, 0.0, OP.is_gt, -32768.0, MUL)
    tt(A("BC"), A("TB1"), A("TB2"), MUL)
    ts(A("TB1"), A("IDF"), 32768.0, MUL)
    tt(A("TB3"), A("TB3"), A("TB2"), MUL)
    copy(A("LN1"), A("LVN"))
    tt(A("EM"), A("TB3"), A("TB1"), ADD)
    lin(A("X0"), A("VROW"), col(cS), col(cBI))

    def late_constants():
        lin(A("MC"), A("M1"), col(cW23))
        lin(A("NBC"), A("BC"), -1.0)
        for name, w in (("IBM", -1.0), ("IDM", -1.0), ("IDE", -float(E))):
            lin(A(name), A("IDF"), w)
        for a, b in THIRDS[1:]:
            act(part("NEG", a, b), part("NEG", 0, 28))

    def mirror(name, a, b):
        dma("y", part("MD", a, b), part(name, a, b))

    HOP = ["P1", "PA", "PB", "PA", "PB", "PA"]
    MW = ["MS", "MA", "MB", "MA", "MB"]
    WW = ["WB", "WA", "WB", "WA", "WB", "TT"]
    PASS = {"DG": ("R", "NEG", True, False), "BC": ("R", "P1", False, True),
            "NBC": ("Q", "HW", True, False), "I32": ("Q", "PA", False, False), "IP": ("Q", "TT", False, True),
            "INJ": ("R", "PB", True, False), "SH": ("R", "TT", False, False), "EM": ("R", "EQ", False, True)}

    def step(name, last):
        wid = E1 if last else E
        lf, up = ("LMX", -E - 15 * UP) if last else ("L1S", UP)
        m32 = "M32B" if last else "M32A"
        low = wid + 16 * UP
        j = int(name[1]) if name[1:2].isdigit() else None
        i = int(name[-1]) if name[-1].isdigit() and (len(name) > 2 or name[0] in "gqky") else None
        a, b = THIRDS[i] if i is not None and i < 3 else (0, C)
        if name == "P1":
            act(A("P1"), G(HWW(0, wid), ul(ENT)))
        elif name[:2] in ("Pv", "Ps"):
            a, b = (0, OPT["p1"]) if name == "Pv" else (OPT["p1"], C)
            (act if name[1] == "s" else copy)(part("P1", a, b), G(HWW(0, wid), ul(ENT, a, b)))
        elif name[:2] in ("Mv", "Ms"):
            (act if name[1] == "s" else copy)(part("MS", a, b), G(A("SPW", 0, wid), ul(ENT, a, b)))
            if last:
                mirror("MS", a, b)
        elif name == "neg":
            ts(A("SPW", E, E1), A("MS"), -1.0, MUL)
        elif name == "snd":
            order("g", [("MB", 0, V), ("MD", 0, V)], [])
            send("SNW", A("SPW", E, E1), E, E1, "arrM")
        elif name == "app":
            if not last:
                for r in (2, 3):
                    dma("y", row(r, E, E1), A("P1", part=ROW[r]))
            order("g", A("UL", PL * C, (PL + 5) * C)[1], [])
            dma("g", A("EW", wid, wid + V, part=ROW[0]), A("P1", part=ROW[2]))
            dma("g", A("EW", wid, wid + V, part=ROW[0]), A("P1", part=ROW[3]), accum_op=ADD)
        elif name == "ENS":
            ts(sm(ENS), si(4), up, ADD)
        elif name == "D":
            mm(ps("Q0", 0, 3), [(A("IDF"), A(lf))], stop=False)
            for k in range(3):
                mm(ps("Q0", k, k + 1), [(A("IDM"), sm(ENS))], start=False, stop=k == 2)
        elif name == "PEN":
            act(A("PEN"), ps("Q0", 0, 3), ACT.Abs, scale=32768.0)
        elif name == "pen":
            mm(ps("Q0", 0, 3), [(A("IBM"), A("PEN"))], stop=False)
        elif name == "MC":
            conv("Q1", "MC", "P1")
        elif name == "NC":
            lin(sm(NC_), *((ps("Q1"), -1.0, UP - low) if last else (sm(ENS), -1.0, 2 * UP - low)))
        elif name == "NV":
            lin(sm(NV), sm(NV), bias=-float(V) if last else -low)
        elif name == "HD":
            act(A("HDF"), A("HDF"), ACT.Silu)
            dma("y", A("YHW", 0, E, part=ROW[0]), A("HDF"))
        elif name == "LF":
            lin(A("LFL"), A(lf), bias=UP - up - low)
        elif name.split("_")[0] in PASS:
            mat = name.split("_")[0]
            bank, src_, start, stop = PASS[mat]
            for k, (a, b) in enumerate(THIRDS):
                if "_" not in name or k == i:
                    x = HWW(E + 16 * a, E + 16 * b) if src_ == "HW" else \
                        part(src_, 0, 28) if src_ == "NEG" else part(src_, a, b)
                    mm(A("%s%d" % (bank, k), 0, 448), [(A(mat), x)], start=start, stop=stop)
        elif name[0] == "c" and j is not None:
            conv("L%d" % (j % 2), "MP", HOP[j])
        elif name[0] == "l" and j is not None:
            copy(ul(PL + j), ps("L%d" % (j % 2)))
        elif name[0] == "h" and j is not None:
            act(part(HOP[j + 1], a, b), G(A(HOP[j]), ul(PL + j, a, b)))
        elif name[0] == "H":
            copy(part(HOP[j + 1], a, b), G(A(HOP[j]), ul(PL + j, a, b)))
        elif name[0] == "m" and j is not None:
            out, neg = (m32 if j == 4 else MW[j + 1]), j == 0 and not last
            tt(part(out, a, b), G(A(MW[j]), ul(PL + j, a, b)), part("SPW", a, b, E) if neg else part("MD", a, b),
               SUB if neg else ADD)
            if j < 3 or j == 3 and "m4%d" % i in ORDER[last]:
                mirror(out, a, b)
        elif name[0] == "w" and j == 0:
            tt(part("WA", a, b), A("R%d" % i, 0, 448), part("X0", a, b), MIN)
        elif name[0] == "w":
            tt(part(WW[j + 1], a, b), G(A(WW[j]), ul(PL + j, a, b)), part("X", a, b), MIN)
        elif name[0] == "x":
            lin(part("X", a, b), part(WW[j], a, b), *((e0, col(cBIG)) if j == 4 else (col(cS + j), col(cBI + j))))
        elif name[0] == "g":
            act(part("MD", a, b), G(A("MB"), ul(PL + 4, a, b)))
        elif name[0] == "q":
            mm(A("L0", 0, 448), [(A("IB"), part(x, a, b)) for x in ("MB", "MD")])
        elif name[0] == "k":
            act(part(m32, a, b), A("L0", 0, 448))
        elif name == "low":
            conv("L1", "M0H", "TT")
        elif name[:2] == "eq":
            ts(part("EQ", a, b), A("Q%d" % i, 0, 448), 0.0, EQL)
        elif name[:2] == "es":
            act(A("AB"), A("Q%d" % i, 0, 448), ACT.Abs)
            act(part("EQ", a, b), A("AB"), ACT.Relu, scale=-1.0, bias=1.0)
        elif name == "min":
            copy(ul(LOWU), ps("L1"))
        elif name[:3] == "pov" or name == "pos0":
            ts(part("POS", a, b), G(A(m32), ul(LOWU, a, b)), 0.5, OP.is_gt, -0.5, ADD)
        elif name[:3] in ("pos", "POS"):
            act(part("POS", a, b), G(A(m32), ul(LOWU, a, b)), ACT.Sign, bias=-0.5)
        elif name[0] == "y":
            ts(part("PD", a, b), A("R%d" % i, 0, 448), -32768.0, ADD, -UP, MAX)
        elif name == "cy":
            conv("L0", "MH", "PD")
        elif name == "cv":
            conv("L1", "MK", "POS")
        elif name == "VV":
            lin(sm(EE), ps("L1"), bias=1.5 * UP - low)
        elif name[:2] == "sc":
            a, b = OPT["sc"][i:i + 2]
            copy(G(A("YSW"), ul(TG1, a, b)), part("SPW", a, b, E))
        else:
            assert name[:2] == "hs", name
            a, b = OPT["hs"][i:i + 2]
            act(G(A("YHW"), ul(TG1, a, b)), part("VROW", a, b), ACT.Silu)

    for rnd in range(2):
        last = rnd == 1
        wid = E1 if last else E
        ln, lf = ("LN2", "LMX") if last else ("LN1", "L1S")
        m32 = "M32B" if last else "M32A"
        KB = {1: "L0", 2: "L1", 0: "Q2"}

        for k in KS:
            mm(ps(KB[k]), [(A(x), A("NEG", 0, C)) for x in ["IDN"] * (k != 2) + ["IDE"] * last] +
               [(A("IDF"), blk(lf, k))], stop=False)
        P9 = [(k, a, b) for k in KS for a, b in THIRDS]
        nh = 0 if last else OPT["help"]
        HB = dict(zip(P9[9 - nh:], ["R0", "R1", "R2", "Q0", "Q1"]))
        for (k, a, b), bank in HB.items():
            mm(A(bank, 0, 448), [(A("IB"), part("SO", a, b, k * V))])
            act(part("YLW", a, b, k * V), G(A("SNW", 0, wid), A(ln, k * C + a, k * C + b)))
        for k in KS:
            own = [x for x in P9 if x[0] == k and x not in HB]
            if own:
                a, b = own[0][1], own[-1][2]
                tt(part("PR", a, b, k * V), G(A("SNW", 0, wid), A(ln, k * C + a, k * C + b)),
                   part("SO", a, b, k * V), MUL)
            for x in HB:
                if x[0] == k:
                    tt(part("PR", x[1], x[2], k * V), A(HB[x], 0, 448), part("YLW", x[1], x[2], k * V), MUL)
            conv(KB[k], "MK", "PR", k * V, start=False)
            if k == 2:
                copy(si(0), ps("L0"))
        if not last:
            late_constants()
            order("y", [("SNW", 0, E)], [])
            dma("y", A("YSW", 0, E), H("sp", T.sp[:]))
        tt(si(1), ps("L1"), si(0), MAX)
        ts(si(2), si(1), -8193, OP.bitwise_and)
        if last and OPT["sc"][3] < C:
            step("sc3", last)
        tt(si(3), ps("Q2"), si(2), MAX)
        ts(si(4), si(3), 8191, OP.bitwise_and)
        copy(ul(ENT), si(4))

        for name in ORDER[rnd].split():
            step(name, last)

        if last:
            dma("g", H("yw", T.yw[:]), A(m32), accum_op=ADD)
        low = wid + 16 * UP
        tt(sm(FF), ps("L0"), sm(EE), MIN)
        for k in range(3):
            mm(ps("Q0", k, k + 1), [(A("IDF"), sm(FF))], start=False, stop=k == 2)
        tg = TG2 if last else TG1
        lu = "LU3" if last else "LU2"
        tt(sm(ZZ), sm(FF), sm(NC_), MIN)
        tt(sm(NT), sm(ZZ), sm(NV), MAX)
        if last:
            ts(ul(tg), sm(NT), -1.0, MUL, UP - low, ADD)
            act(G(A("YHW"), ul(tg)), A("VROW"), ACT.Silu)
            dma("s", A("HDF"), A("YHW", 0, E, part=ROW[0]))
            if not OPT["lu_first"]:
                tt(G(A("YSW"), ul(tg)), A("MS"), A("NEG"), MUL)
        tt(A("LMX"), ps("Q0", 0, 3), A("LFL"), MAX)
        ts(A(lu), A("LMX"), low - UP, ADD)
        if not last:
            send("LN2", A("LU2"), 0, 252, "arrN")
            for k in KS:
                act(blk("SO", k, V), G(A("SPW"), blk("LU2", k)))
            ts(ul(tg), sm(NT), -1.0, MUL, UP - low, ADD)
            dma("g", H("yw", T.yw[:]), A(m32))
            for name in AFTER.split():
                step(name, last)
        else:
            if OPT["lu_first"]:
                tt(G(A("YSW"), ul(tg)), A("MS"), A("NEG"), MUL)
            dma("y", H("ys", T.ys[:]), A("YSW", 0, E))
            for f, q, a, b in ((act, "s", 0, OPT["yl"]), (copy, "y", OPT["yl"], OPT["yh"]), (copy, "y", OPT["yh"], 252)):
                if a == OPT["yh"]:
                    ts(A("HR1"), A("HDF"), 12582912.0, ADD, -12582976.0, ADD)
                    dma("y", H("yh", T.yh[:]), A("HR1"))
                if a < b:
                    f(A("YLW", 16 * a, 16 * b), G(A("EW"), A("LU3", a, b)))
                    dma(q, H("yl%d" % a, T.yl[:, 16 * a:16 * b]), A("YLW", 16 * a, 16 * b, part=ROW[0]))

    total["sent"] = sent[0]
    for s in sorted(total):
        wait("g", (s, total[s], {}))
